import numpy as np
import ml_dtypes


def mxq(x, axis, fmt="e4m3"):
    dtype, down = {"e4m3": (ml_dtypes.float8_e4m3fn, 7), "e5m2": (ml_dtypes.float8_e5m2, 14)}[fmt]
    v = np.moveaxis(np.asarray(x, np.float32).astype(ml_dtypes.bfloat16).astype(np.float64), axis, -1)
    blocks = v.reshape(v.shape[:-1] + (-1, 32))
    amax = np.abs(blocks).max(-1, keepdims=True)
    byte = np.maximum(np.where(amax > 0, np.frexp(amax)[1] - 1 + 127, 0) - down, 1)
    scale = np.exp2(byte - 127.0)
    codes = (blocks / scale).astype(np.float32).astype(dtype).astype(np.float64)
    return np.moveaxis((codes * scale).reshape(v.shape), -1, axis)


WIDE = False


def mx_kscale(k):
    if not WIDE:
        return np.ones(k)
    levels = np.array([10, -10, 5, -5, 0])
    if k % 512:
        return np.exp2(np.random.permutation(np.resize(levels, k // 32))).repeat(32)
    a = np.empty((k // 512, 16))
    for p in range(k // 512):
        a[p, :8] = np.random.permutation(np.resize(levels, 8))
        for g in range(8):
            far = levels[np.abs(levels - a[p, g]) >= 10]
            a[p, g + 8] = far[np.random.randint(len(far))]
    return np.exp2(a.ravel()).repeat(32)


def f64(x):
    return np.asarray(x).astype(np.float64)


def striped(idx):
    return np.tile(idx.reshape(-1, 16).T, (8, 1)).astype(np.uint16)


def unstriped(offs):
    return offs[:16].T.reshape(-1).astype(np.int64)


E2M1 = np.array([0.0, 0.5, 1.0, 1.5, 2.0, 3.0, 4.0, 6.0, -0.0, -0.5, -1.0, -1.5, -2.0, -3.0, -4.0, -6.0])


def pack_weight(w, fmt):
    k, n = w.shape
    w = f64(np.asarray(w, np.float32).astype(ml_dtypes.bfloat16)).reshape(k // 32, 32, n)
    amax = np.abs(w).max(1)
    if fmt == "e4m3":
        byte = np.frexp(amax)[1] - 1 + 127 - 7
    else:
        mant, ex = np.frexp(amax / 6.0)
        byte = np.where(mant > 0.5, ex, ex - 1) + 127
    byte = np.clip(np.where(amax > 0, byte, 1), 1, 254)
    scaled = (w * np.exp2(127.0 - byte)[:, None, :]).reshape(k, n).astype(np.float32)
    by_word = np.ascontiguousarray(scaled.reshape(k // 512, 128, 4, n).transpose(0, 1, 3, 2))
    if fmt == "e4m3":
        words = by_word.astype(ml_dtypes.float8_e4m3fn).view(np.uint8)
    else:
        c = by_word.astype(ml_dtypes.float4_e2m1fn).view(np.uint8) & 0xF
        words = (c[..., 0::2] | (c[..., 1::2] << 4)).reshape(k // 512, 128, 2 * n)
    return np.ascontiguousarray(words), np.ascontiguousarray(byte.astype(np.uint8).reshape(k // 512, 16, n))


def unpack_weight(words, scales, fmt):
    g, _, n = scales.shape
    words = np.ascontiguousarray(words).reshape(g, 128, n, -1)
    if fmt == "e4m3":
        vals = words.view(ml_dtypes.float8_e4m3fn).astype(np.float64)
    else:
        nib = np.empty((g, 128, n, 4), np.uint8)
        nib[..., 0::2] = words & 0xF
        nib[..., 1::2] = words >> 4
        vals = E2M1[nib]
    vals = vals * np.repeat(np.exp2(scales.astype(np.float64) - 127.0), 8, axis=1)[..., None]
    return vals.transpose(0, 1, 3, 2).reshape(g * 512, n)


def gelu(v):
    return 0.5 * v * (1.0 + np.tanh(np.sqrt(2.0 / np.pi) * (v + 0.044715 * v**3)))


def bf(x):
    return np.asarray(x, np.float32).astype(ml_dtypes.bfloat16)

def planes(Y):
    n, m = Y.shape
    b = f64(bf(Y)).reshape(n // 32, 32, m)
    amax = np.abs(b).max(1)
    byte = np.clip(np.where(amax > 0, np.frexp(amax)[1] - 1 + 127 - 7, 1), 1, 254)
    codes = (b * np.exp2(127.0 - byte)[:, None, :]).reshape(n, m).astype(np.float32).astype(ml_dtypes.float8_e4m3fn).view(np.uint8)
    words = codes.reshape(n // 512, 128, 4, m).transpose(0, 1, 3, 2)
    return np.ascontiguousarray(words), np.ascontiguousarray(byte.astype(np.uint8).reshape(n // 512, 16, m))


K, H, N, T, S, P = 1024, 1024, 512, 4096, 1024, 512

def setup_inputs():
    n = lambda *shape: np.random.standard_normal(shape)
    s = mx_kscale(K)[:, None]
    u = mx_kscale(H)[:, None]
    tab_words, tab_scales = pack_weight(n(K, T) * s, "e4m3")
    w1_words, w1_scales = pack_weight(n(K, H) / np.sqrt(K) / s * u.T, "e2m1")
    return {
        "tab_words": tab_words, "tab_scales": tab_scales,
        "w1_words": w1_words, "w1_scales": w1_scales,
        "wg": (1.5 * n(K, N) / np.sqrt(K) / s).astype(np.float32),
        "w2": (0.7 * n(H, N) / np.sqrt(H) / u).astype(np.float32),
        "gain": (2.0 * np.exp(0.8 * n(N))).astype(np.float32),
        "offs": striped(np.random.permutation(T)[:S]),
        "pos1": striped(np.random.permutation(S)[:P]),
        "pos2": striped(np.random.permutation(S)[:P]),
    }

def reference(tab_words, tab_scales, w1_words, w1_scales, wg, w2, gain, offs, pos1, pos2):
    v = unpack_weight(tab_words, tab_scales, "e4m3")[:, unstriped(offs)]
    w1 = unpack_weight(w1_words, w1_scales, "e2m1")
    h = w1.T @ v
    q = mxq(f64(wg), 0, "e4m3").T @ v
    a = h[:, unstriped(pos1)]
    b = h[:, unstriped(pos2)]
    z = a + b
    m = mxq(f64(w2), 0, "e4m3").T @ mxq(z, 0, "e4m3")
    gate = 1.0 / (1.0 + np.exp(-q[:, unstriped(pos1)]))
    y = f64(gain)[:, None] * (np.tanh(m) * gate)
    words, scales = planes(y)
    return y, words, scales

@@ -1,0 +1,277 @@
+from contextlib import ExitStack
+
+import concourse.mybir as mybir
+
+K, H, N, T, S, NODES = 1024, 1024, 512, 4096, 1024, 512
+FLOPS = 2 * K * H * S + 2 * K * N * S + 2 * H * N * NODES
+
+F32 = mybir.dt.float32
+BF16 = mybir.dt.bfloat16
+I32 = mybir.dt.int32
+U32 = mybir.dt.uint32
+U16 = mybir.dt.uint16
+U8 = mybir.dt.uint8
+FP8X4 = mybir.dt.float8_e4m3fn_x4
+FP4X4 = mybir.dt.float4_e2m1fn_x4
+MULT = mybir.AluOpType.mult
+ADD = mybir.AluOpType.add
+SIGMOID = mybir.ActivationFunctionType.Sigmoid
+TANH = mybir.ActivationFunctionType.Tanh
+
+P = 128
+PACK = 4
+PASS_K = P * PACK
+BANK = 512
+HALF = NODES // 2
+ALIGN = 64
+
+
+def tile_list_syntax_pair_compose_kernel(
+    tc, tab_words, tab_scales, w1_words, w1_scales, wg, w2, gain, offs, pos1, pos2, out_0, out_1, out_2
+):
+    nc = tc.nc
+    with ExitStack() as ctx:
+        lists = ctx.enter_context(tc.tile_pool(name="lists", bufs=1))
+        keep = ctx.enter_context(tc.tile_pool(name="keep", bufs=1))
+        ring = ctx.enter_context(tc.tile_pool(name="ring", bufs=4))
+        psum = ctx.enter_context(tc.psum_pool(name="psum", bufs=8))
+
+        def held(shape, dtype, name, tag=None):
+            return keep.tile(shape, dtype, name=name, tag=tag or name, align_bytes=ALIGN)
+
+        offs_sb = lists.tile([P, S // 16], U16, name="offs_sb")
+        pos1_sb = lists.tile([P, NODES // 16], U16, name="pos1_sb")
+        pos2_sb = lists.tile([P, NODES // 16], U16, name="pos2_sb")
+        nc.sync.dma_start(offs_sb[:], offs)
+        nc.sync.dma_start(pos1_sb[:], pos1)
+        nc.sync.dma_start(pos2_sb[:], pos2)
+
+        scale_window = held([P, T], U8, "scale_window", "slot_wg0")
+        nc.vector.memset(scale_window[:].bitcast(I32), 0)
+        for quad in range(4):
+            nc.scalar.dma_start(
+                scale_window[32 * quad : 32 * quad + 8, :].bitcast(I32),
+                tab_scales[:, 4 * quad : 4 * quad + 4, :].bitcast(I32),
+            )
+
+        w1s_raw = held([P, 2 * H], U8, "w1s_raw", "slot_w2_1")
+        nc.gpsimd.memset(w1s_raw[:].bitcast(I32), 0)
+        for quad in range(4):
+            nc.gpsimd.dma_start(
+                w1s_raw[32 * quad : 32 * quad + 4, :].bitcast(I32).rearrange("r (a c) -> r a c", a=2),
+                w1_scales[:, 4 * quad : 4 * quad + 4, :].bitcast(I32).rearrange("a r c -> r a c"),
+            )
+        gain_sb = held([P, PACK], F32, "gain_sb")
+        nc.gpsimd.dma_start(gain_sb[:], gain.rearrange("(p t) -> p t", t=PACK))
+
+        word_window = [held([P, T], I32, "word_window0", "slot_w2_0"), held([P, T], I32, "word_window1")]
+        w1w_raw = held([P, H], I32, "w1w_raw", "slot_wg1")
+        nc.sync.dma_start(word_window[0][:], tab_words[0].rearrange("p t i -> p (t i)").bitcast(I32))
+        nc.sync.dma_start(
+            w1w_raw[:].rearrange("p (a c) -> p a c", a=2), w1_words.bitcast(I32).rearrange("a p c -> p a c")
+        )
+        nc.sync.dma_start(word_window[1][:], tab_words[1].rearrange("p t i -> p (t i)").bitcast(I32))
+
+        v_scales0 = held([P, S], U8, "v_scales0")
+        nc.vector.tensor_copy(v_scales0[:], scale_window[:].indirect(offs_sb[:]))
+        v_scales1 = held([P, S], U8, "v_scales1")
+        nc.gpsimd.memset(v_scales1[96:128, :].bitcast(I32), 0)
+        nc.scalar.dma_start(v_scales1[0:112, :].bitcast(I32), v_scales0[4:116, :].bitcast(I32))
+        v_scales = [v_scales0, v_scales1]
+
+        w1_codes = held([P, 2 * 2 * H], U8, "w1_codes")
+        nc.vector.tensor_copy(
+            w1_codes[:].bitcast(I32).rearrange("p (ab s g w) -> p ab s g w", ab=4, s=PACK, w=4),
+            w1w_raw[:].rearrange("p (ab g s w) -> p ab s g w", ab=4, s=PACK, w=4),
+        )
+        w1_scale = held([P, 2 * H], U8, "w1_scale")
+        nc.vector.tensor_copy(
+            w1_scale[:].bitcast(I32).rearrange("p (ab s g w) -> p ab s g w", ab=4, s=PACK, w=2),
+            w1s_raw[:].bitcast(I32).rearrange("p (ab g s w) -> p ab s g w", ab=4, s=PACK, w=2),
+        )
+
+        v_words0 = held([P, S], I32, "v_words0")
+        nc.vector.tensor_copy(v_words0[:].bitcast(U32), word_window[0][:].bitcast(U32).indirect(offs_sb[:]))
+        v_words = {(0, 0): v_words0[:, 0:BANK], (0, 1): v_words0[:, BANK:S]}
+        for j in range(2):
+            part = held([P, BANK], I32, "v_words1_%d" % j)
+            nc.vector.tensor_copy(
+                part[:].bitcast(U32), word_window[1][:].bitcast(U32).indirect(offs_sb[:, 32 * j : 32 * (j + 1)])
+            )
+            v_words[(1, j)] = part[:]
+
+        wg_raw = [held([P, PACK, N], F32, "wg_raw%d" % a, "slot_wg%d" % a) for a in range(2)]
+        w2_raw = [held([P, PACK, N], F32, "w2_raw%d" % b, "slot_w2_%d" % b) for b in range(2)]
+        for a in range(2):
+            nc.sync.dma_start(
+                wg_raw[a][:], wg[a * PASS_K : (a + 1) * PASS_K, :].rearrange("(p j) n -> p j n", j=PACK)
+            )
+        for b in range(2):
+            rows = w2[b * PASS_K : (b + 1) * PASS_K, :].rearrange("(g s e) n -> s g e n", s=PACK, e=8)
+            for s in range(PACK):
+                nc.sync.dma_start(w2_raw[b][:, s, :], rows[s])
+
+        def round_weight(copy, raw, name, tag):
+            rounded = held([P, PACK * N], BF16, name, tag)
+            copy(
+                rounded[:].rearrange("p (u e m j) -> p u m j e", u=2, e=2, j=PACK),
+                raw[:].rearrange("p j (m u e) -> p u m j e", u=2, e=2),
+            )
+            return rounded
+
+        def quantize(rounded, name):
+            width = rounded.shape[1] // PACK
+            codes = held([P, width], U32, name + "_codes")
+            scales = held([P, width], U8, name + "_scales")
+            nc.vector.quantize_mx(out=codes[:].bitcast(FP8X4), scales=scales[:], in_=rounded[:])
+            return codes, scales
+
+        wg_mx = [quantize(round_weight(nc.vector.tensor_copy, wg_raw[0], "wg_bf0", "wg_bf0"), "wg0")]
+
+        def token_pass(acc, codes, scales, a, j):
+            nc.tensor.matmul_mx(
+                out=acc[:],
+                lhsT=codes,
+                lhsT_scale=scales,
+                rhs=v_words[(a, j)].bitcast(FP8X4),
+                rhs_scale=v_scales[a][:, j * BANK : (j + 1) * BANK],
+                start=(a == 0),
+                stop=(a == 1),
+            )
+
+        def h_pass(acc, tile, a, j):
+            col = a * H + tile * P
+            token_pass(
+                acc, w1_codes[:, 2 * col : 2 * (col + P)].bitcast(FP4X4), w1_scale[:, col : col + P], a, j
+            )
+
+        h = [held([P, S], F32, "h%d" % tile) for tile in range(8)]
+        h_acc = {}
+        for tile in range(4):
+            for j in range(2):
+                h_acc[(tile, j)] = psum.tile([P, BANK], F32, name="acc")
+                h_pass(h_acc[(tile, j)], tile, 0, j)
+        for tile in range(8):
+            for j in range(2):
+                if tile >= 4:
+                    h_acc[(tile, j)] = psum.tile([P, BANK], F32, name="acc")
+                    h_pass(h_acc[(tile, j)], tile, 0, j)
+                h_pass(h_acc[(tile, j)], tile, 1, j)
+                nc.scalar.copy(h[tile][:, j * BANK : (j + 1) * BANK], h_acc[(tile, j)][:])
+
+        def node_slice(pos, half):
+            return pos[:, half * (HALF // 16) : (half + 1) * (HALF // 16)]
+
+        def sum_children(units, z):
+            first = []
+            for n in range(len(units) + 1):
+                if n < len(units):
+                    tile, half = units[n]
+                    child = ring.tile([P, HALF], F32, name="child")
+                    nc.vector.tensor_copy(child[:], h[tile][:].indirect(node_slice(pos1_sb, half)))
+                    first.append(child)
+                if n > 0:
+                    tile, half = units[n - 1]
+                    nc.vector.tensor_tensor(
+                        z[half][:, tile % PACK, :], h[tile][:].indirect(node_slice(pos2_sb, half)), first[n - 1][:], ADD
+                    )
+
+        def interleave(copy, rows, name, tag):
+            rounded = held([P, PACK * HALF], BF16, name, tag)
+            copy(
+                rounded[:].rearrange("p (c i s) -> p c s i", i=4, s=PACK),
+                rows[:].rearrange("p s (c i) -> p c s i", i=4),
+            )
+            return rounded
+
+        z0 = [held([P, PACK, HALF], F32, "z0_%d" % half) for half in range(2)]
+        sum_children([(tile, half) for tile in range(4) for half in range(2)], z0)
+
+        wg_mx.append(quantize(round_weight(nc.scalar.copy, wg_raw[1], "wg_bf1", "slot_z1_0"), "wg1"))
+        z1 = {0: held([P, PACK, HALF], F32, "z1_0", "slot_z1_0")}
+        sum_children([(tile, 0) for tile in range(4, 8)], z1)
+
+        w2_mx = [
+            quantize(round_weight(nc.scalar.copy, w2_raw[0], "w2_bf0", "w2_bf0"), "w2_0"),
+            quantize(round_weight(nc.scalar.copy, w2_raw[1], "w2_bf1", "slot_z1_1"), "w2_1"),
+        ]
+        z1[1] = held([P, PACK, HALF], F32, "z1_1", "slot_z1_1")
+        sum_children([(tile, 1) for tile in range(4, 8)], z1)
+
+        z_mx = {}
+        for half in range(2):
+            name = "z0_bf%d" % half
+            z_mx[(0, half)] = quantize(interleave(nc.scalar.copy, z0[half], name, name), name)
+
+        q = [held([P, S], F32, "q%d" % t) for t in range(PACK)]
+        for t in range(PACK):
+            for j in range(2):
+                acc = psum.tile([P, BANK], F32, name="acc")
+                for a in range(2):
+                    codes, scales = wg_mx[a]
+                    token_pass(acc, codes[:, t * P : (t + 1) * P].bitcast(FP8X4), scales[:, t * P : (t + 1) * P], a, j)
+                nc.scalar.copy(q[t][:, j * BANK : (j + 1) * BANK], acc[:])
+
+        gate = []
+
+        def gate_rows(t, tag):
+            logits = held([P, NODES], F32, "logits%d" % t, tag)
+            nc.vector.tensor_copy(logits[:], q[t][:].indirect(pos1_sb[:]))
+            gate_t = held([P, NODES], F32, "gate%d" % t)
+            nc.scalar.activation(gate_t[:], logits[:], SIGMOID)
+            gate.append(gate_t)
+
+        tanh_m = {}
+
+        def compose(half):
+            for pair in range(2):
+                acc = psum.tile([P, 2, HALF], F32, name="acc")
+                for e in range(2):
+                    t = 2 * pair + e
+                    for b in range(2):
+                        w_codes, w_scales = w2_mx[b]
+                        z_codes, z_scales = z_mx[(b, half)]
+                        nc.tensor.matmul_mx(
+                            out=acc[:, e, :],
+                            lhsT=w_codes[:, t * P : (t + 1) * P].bitcast(FP8X4),
+                            lhsT_scale=w_scales[:, t * P : (t + 1) * P],
+                            rhs=z_codes[:].bitcast(FP8X4),
+                            rhs_scale=z_scales[:],
+                            start=(b == 0),
+                            stop=(b == 1),
+                        )
+                squashed = held([P, 2, HALF], F32, "tanh_m%d_%d" % (half, pair))
+                nc.scalar.activation(squashed[:], acc[:], TANH)
+                tanh_m[(half, pair)] = squashed
+
+        z1_rounded = [
+            interleave(nc.scalar.copy, z1[half], "z1_bf%d" % half, "slot_logits%d" % (2 + half)) for half in range(2)
+        ]
+        gate_rows(0, "logits0")
+        gate_rows(1, "logits1")
+        for half in range(2):
+            z_mx[(1, half)] = quantize(z1_rounded[half], "z1_bf%d" % half)
+            gate_rows(2 + half, "slot_logits%d" % (2 + half))
+            compose(half)
+
+        y_scales = held([P, NODES], U8, "y_scales")
+        y_rows = out_0.rearrange("(p t) i -> p t i", t=PACK)
+        code_rows = out_1[0].rearrange("p i t -> p (i t)").bitcast(I32)
+        for half in range(2):
+            cols = slice(half * HALF, (half + 1) * HALF)
+            y = held([P, PACK, HALF], F32, "y%d" % half)
+            for t in range(PACK):
+                nc.vector.scalar_tensor_tensor(
+                    y[:, t, :], tanh_m[(half, t // 2)][:, t % 2, :], gain_sb[:, t : t + 1], gate[t][:, cols], MULT, MULT
+                )
+            nc.sync.dma_start(y_rows[:, :, cols], y[:])
+            name = "y_bf%d" % half
+            rounded = interleave(nc.vector.tensor_copy, y, name, name)
+            y_codes = held([P, HALF], I32, "y_codes%d" % half)
+            nc.vector.quantize_mx(out=y_codes[:].bitcast(FP8X4), scales=y_scales[:, cols], in_=rounded[:])
+            nc.sync.dma_start(code_rows[:, cols], y_codes[:])
+        for quad in range(4):
+            queue = nc.scalar if quad % 2 else nc.sync
+            queue.dma_start(
+                out_2[0, 4 * quad : 4 * quad + 4, :].bitcast(I32), y_scales[32 * quad : 32 * quad + 4, :].bitcast(I32)
+            )

@@ -46,31 +46,43 @@ def tile_list_syntax_pair_compose_kernel(
         nc.sync.dma_start(pos1_sb[:], pos1)
         nc.sync.dma_start(pos2_sb[:], pos2)
 
-        scale_window = held([P, T], U8, "scale_window", "slot_wg0")
-        nc.vector.memset(scale_window[:].bitcast(I32), 0)
-        for quad in range(4):
-            nc.scalar.dma_start(
-                scale_window[32 * quad : 32 * quad + 8, :].bitcast(I32),
-                tab_scales[:, 4 * quad : 4 * quad + 4, :].bitcast(I32),
-            )
-
         w1s_raw = held([P, 2 * H], U8, "w1s_raw", "slot_w2_1")
-        nc.gpsimd.memset(w1s_raw[:].bitcast(I32), 0)
         for quad in range(4):
-            nc.gpsimd.dma_start(
+            nc.sync.dma_start(
                 w1s_raw[32 * quad : 32 * quad + 4, :].bitcast(I32).rearrange("r (a c) -> r a c", a=2),
                 w1_scales[:, 4 * quad : 4 * quad + 4, :].bitcast(I32).rearrange("a r c -> r a c"),
             )
-        gain_sb = held([P, PACK], F32, "gain_sb")
-        nc.gpsimd.dma_start(gain_sb[:], gain.rearrange("(p t) -> p t", t=PACK))
-
         word_window = [held([P, T], I32, "word_window0", "slot_w2_0"), held([P, T], I32, "word_window1")]
+        word_rows = [tab_words[a].rearrange("p t i -> p (t i)").bitcast(I32) for a in range(2)]
+        nc.sync.dma_start(word_window[0][:, 0 : T // 2], word_rows[0][:, 0 : T // 2])
+        gain_sb = held([P, PACK], F32, "gain_sb")
+        nc.sync.dma_start(gain_sb[:], gain.rearrange("(p t) -> p t", t=PACK))
+
+        scale_window = held([P, T], U8, "scale_window", "slot_wg0")
+        nc.vector.memset(scale_window[:].bitcast(I32), 0)
+        for quad in range(4):
+            nc.sync.dma_start(
+                scale_window[32 * quad : 32 * quad + 8, :].bitcast(I32),
+                tab_scales[:, 4 * quad : 4 * quad + 4, :].bitcast(I32),
+            )
+        nc.sync.dma_start(word_window[0][:, T // 2 : T], word_rows[0][:, T // 2 : T])
         w1w_raw = held([P, H], I32, "w1w_raw", "slot_wg1")
-        nc.sync.dma_start(word_window[0][:], tab_words[0].rearrange("p t i -> p (t i)").bitcast(I32))
         nc.sync.dma_start(
             w1w_raw[:].rearrange("p (a c) -> p a c", a=2), w1_words.bitcast(I32).rearrange("a p c -> p a c")
         )
-        nc.sync.dma_start(word_window[1][:], tab_words[1].rearrange("p t i -> p (t i)").bitcast(I32))
+        nc.sync.dma_start(word_window[1][:], word_rows[1])
+
+        warm = held([P, PACK], F32, "warm")
+        nc.scalar.activation(warm[:], gain_sb[:], SIGMOID)
+
+        w1_scale = held([P, 2 * H], U8, "w1_scale")
+        nc.gpsimd.memset(w1_scale[:].bitcast(I32), 0)
+        for quad in range(4):
+            live = slice(32 * quad, 32 * quad + 4)
+            nc.vector.tensor_copy(
+                w1_scale[live, :].bitcast(I32).rearrange("p (ab s g w) -> p ab s g w", ab=4, s=PACK, w=2),
+                w1s_raw[live, :].bitcast(I32).rearrange("p (ab g s w) -> p ab s g w", ab=4, s=PACK, w=2),
+            )
 
         v_scales0 = held([P, S], U8, "v_scales0")
         nc.vector.tensor_copy(v_scales0[:], scale_window[:].indirect(offs_sb[:]))
@@ -79,20 +91,14 @@ def tile_list_syntax_pair_compose_kernel(
         nc.scalar.dma_start(v_scales1[0:112, :].bitcast(I32), v_scales0[4:116, :].bitcast(I32))
         v_scales = [v_scales0, v_scales1]
 
+        v_words0 = held([P, S], I32, "v_words0")
+        nc.vector.tensor_copy(v_words0[:].bitcast(U32), word_window[0][:].bitcast(U32).indirect(offs_sb[:]))
+        v_words = {(0, 0): v_words0[:, 0:BANK], (0, 1): v_words0[:, BANK:S]}
         w1_codes = held([P, 2 * 2 * H], U8, "w1_codes")
         nc.vector.tensor_copy(
             w1_codes[:].bitcast(I32).rearrange("p (ab s g w) -> p ab s g w", ab=4, s=PACK, w=4),
             w1w_raw[:].rearrange("p (ab g s w) -> p ab s g w", ab=4, s=PACK, w=4),
         )
-        w1_scale = held([P, 2 * H], U8, "w1_scale")
-        nc.vector.tensor_copy(
-            w1_scale[:].bitcast(I32).rearrange("p (ab s g w) -> p ab s g w", ab=4, s=PACK, w=2),
-            w1s_raw[:].bitcast(I32).rearrange("p (ab g s w) -> p ab s g w", ab=4, s=PACK, w=2),
-        )
-
-        v_words0 = held([P, S], I32, "v_words0")
-        nc.vector.tensor_copy(v_words0[:].bitcast(U32), word_window[0][:].bitcast(U32).indirect(offs_sb[:]))
-        v_words = {(0, 0): v_words0[:, 0:BANK], (0, 1): v_words0[:, BANK:S]}
         for j in range(2):
             part = held([P, BANK], I32, "v_words1_%d" % j)
             nc.vector.tensor_copy(
@@ -179,8 +185,8 @@ def tile_list_syntax_pair_compose_kernel(
         def interleave(copy, rows, name, tag):
             rounded = held([P, PACK * HALF], BF16, name, tag)
             copy(
-                rounded[:].rearrange("p (c i s) -> p c s i", i=4, s=PACK),
-                rows[:].rearrange("p s (c i) -> p c s i", i=4),
+                rounded[:].rearrange("p (c i s) -> p c s i", i=2, s=PACK),
+                rows[:].rearrange("p s (c i) -> p c s i", i=2),
             )
             return rounded
 
@@ -266,7 +272,7 @@ def tile_list_syntax_pair_compose_kernel(
                 )
             nc.sync.dma_start(y_rows[:, :, cols], y[:])
             name = "y_bf%d" % half
-            rounded = interleave(nc.vector.tensor_copy, y, name, name)
+            rounded = interleave(nc.vector.tensor_copy if half else nc.scalar.copy, y, name, name)
             y_codes = held([P, HALF], I32, "y_codes%d" % half)
             nc.vector.quantize_mx(out=y_codes[:].bitcast(FP8X4), scales=y_scales[:, cols], in_=rounded[:])
             nc.sync.dma_start(code_rows[:, cols], y_codes[:])

@@ -46,27 +46,23 @@ def tile_list_syntax_pair_compose_kernel(
         nc.sync.dma_start(pos1_sb[:], pos1)
         nc.sync.dma_start(pos2_sb[:], pos2)
 
-        w1s_raw = held([P, 2 * H], U8, "w1s_raw", "slot_w2_1")
-        for quad in range(4):
-            nc.sync.dma_start(
-                w1s_raw[32 * quad : 32 * quad + 4, :].bitcast(I32).rearrange("r (a c) -> r a c", a=2),
-                w1_scales[:, 4 * quad : 4 * quad + 4, :].bitcast(I32).rearrange("a r c -> r a c"),
-            )
+        w1s_raw = held([P, 2 * H], U8, "w1s_raw")
+        w1s_rows = w1_scales.bitcast(I32).rearrange("a (q r) c -> r q a c", r=4)
+        for r in range(4):
+            nc.sync.dma_start(w1s_raw[r:P:32, :].bitcast(I32).rearrange("q (a c) -> q a c", a=2), w1s_rows[r])
         word_window = [held([P, T], I32, "word_window0", "slot_w2_0"), held([P, T], I32, "word_window1")]
         word_rows = [tab_words[a].rearrange("p t i -> p (t i)").bitcast(I32) for a in range(2)]
         nc.sync.dma_start(word_window[0][:, 0 : T // 2], word_rows[0][:, 0 : T // 2])
         gain_sb = held([P, PACK], F32, "gain_sb")
         nc.sync.dma_start(gain_sb[:], gain.rearrange("(p t) -> p t", t=PACK))
 
-        scale_window = held([P, T], U8, "scale_window", "slot_wg0")
+        scale_window = held([P, T], U8, "scale_window", "slot_wg")
         nc.vector.memset(scale_window[:].bitcast(I32), 0)
-        for quad in range(4):
-            nc.sync.dma_start(
-                scale_window[32 * quad : 32 * quad + 8, :].bitcast(I32),
-                tab_scales[:, 4 * quad : 4 * quad + 4, :].bitcast(I32),
-            )
+        scale_rows = tab_scales.bitcast(I32).rearrange("a (q r) c -> r q a c", r=4)
+        for r in range(4):
+            nc.sync.dma_start(scale_window[r:P:16, :].bitcast(I32), scale_rows[r])
         nc.sync.dma_start(word_window[0][:, T // 2 : T], word_rows[0][:, T // 2 : T])
-        w1w_raw = held([P, H], I32, "w1w_raw", "slot_wg1")
+        w1w_raw = held([P, H], I32, "w1w_raw", "slot_w2_1")
         nc.sync.dma_start(
             w1w_raw[:].rearrange("p (a c) -> p a c", a=2), w1_words.bitcast(I32).rearrange("a p c -> p a c")
         )
@@ -88,7 +84,7 @@ def tile_list_syntax_pair_compose_kernel(
         nc.vector.tensor_copy(v_scales0[:], scale_window[:].indirect(offs_sb[:]))
         v_scales1 = held([P, S], U8, "v_scales1")
         nc.gpsimd.memset(v_scales1[96:128, :].bitcast(I32), 0)
-        nc.scalar.dma_start(v_scales1[0:112, :].bitcast(I32), v_scales0[4:116, :].bitcast(I32))
+        nc.sync.dma_start(v_scales1[0:112, :].bitcast(I32), v_scales0[16:128, :].bitcast(I32))
         v_scales = [v_scales0, v_scales1]
 
         v_words0 = held([P, S], I32, "v_words0")
@@ -106,24 +102,23 @@ def tile_list_syntax_pair_compose_kernel(
             )
             v_words[(1, j)] = part[:]
 
-        wg_raw = [held([P, PACK, N], F32, "wg_raw%d" % a, "slot_wg%d" % a) for a in range(2)]
+        wg_both = held([P, 2 * PACK * N], F32, "wg_raw", "slot_wg")
+        wg_raw = [wg_both[:, a * PACK * N : (a + 1) * PACK * N].rearrange("p (j n) -> p j n", j=PACK) for a in range(2)]
         w2_raw = [held([P, PACK, N], F32, "w2_raw%d" % b, "slot_w2_%d" % b) for b in range(2)]
         for a in range(2):
             nc.sync.dma_start(
-                wg_raw[a][:], wg[a * PASS_K : (a + 1) * PASS_K, :].rearrange("(p j) n -> p j n", j=PACK)
+                wg_raw[a], wg[a * PASS_K : (a + 1) * PASS_K, :].rearrange("(p j) n -> p j n", j=PACK)
             )
         for b in range(2):
             rows = w2[b * PASS_K : (b + 1) * PASS_K, :].rearrange("(g s e) n -> s g e n", s=PACK, e=8)
             for s in range(PACK):
                 nc.sync.dma_start(w2_raw[b][:, s, :], rows[s])
 
-        def round_weight(copy, raw, name, tag):
-            rounded = held([P, PACK * N], BF16, name, tag)
+        def round_weight(copy, raw, rounded):
             copy(
-                rounded[:].rearrange("p (u e m j) -> p u m j e", u=2, e=2, j=PACK),
-                raw[:].rearrange("p j (m u e) -> p u m j e", u=2, e=2),
+                rounded.rearrange("p (u e m j) -> p u m j e", u=2, e=2, j=PACK),
+                raw.rearrange("p j (m u e) -> p u m j e", u=2, e=2),
             )
-            return rounded
 
         def quantize(rounded, name):
             width = rounded.shape[1] // PACK
@@ -132,7 +127,8 @@ def tile_list_syntax_pair_compose_kernel(
             nc.vector.quantize_mx(out=codes[:].bitcast(FP8X4), scales=scales[:], in_=rounded[:])
             return codes, scales
 
-        wg_mx = [quantize(round_weight(nc.vector.tensor_copy, wg_raw[0], "wg_bf0", "wg_bf0"), "wg0")]
+        wg_rounded = held([P, 2 * PACK * N], BF16, "wg_rounded", "slot_z1_0")
+        round_weight(nc.vector.tensor_copy, wg_raw[0], wg_rounded[:, 0 : PACK * N])
 
         def token_pass(acc, codes, scales, a, j):
             nc.tensor.matmul_mx(
@@ -179,43 +175,48 @@ def tile_list_syntax_pair_compose_kernel(
                 if n > 0:
                     tile, half = units[n - 1]
                     nc.vector.tensor_tensor(
-                        z[half][:, tile % PACK, :], h[tile][:].indirect(node_slice(pos2_sb, half)), first[n - 1][:], ADD
+                        z(tile % PACK, half), h[tile][:].indirect(node_slice(pos2_sb, half)), first[n - 1][:], ADD
                     )
 
         def interleave(copy, rows, name, tag):
-            rounded = held([P, PACK * HALF], BF16, name, tag)
+            rounded = held([P, PACK * rows.shape[2]], BF16, name, tag)
             copy(
                 rounded[:].rearrange("p (c i s) -> p c s i", i=2, s=PACK),
                 rows[:].rearrange("p s (c i) -> p c s i", i=2),
             )
             return rounded
 
-        z0 = [held([P, PACK, HALF], F32, "z0_%d" % half) for half in range(2)]
-        sum_children([(tile, half) for tile in range(4) for half in range(2)], z0)
+        z0 = held([P, PACK, NODES], F32, "z0")
+        sum_children(
+            [(tile, half) for tile in range(4) for half in range(2)],
+            lambda s, half: z0[:, s, half * HALF : (half + 1) * HALF],
+        )
 
-        wg_mx.append(quantize(round_weight(nc.scalar.copy, wg_raw[1], "wg_bf1", "slot_z1_0"), "wg1"))
+        round_weight(nc.scalar.copy, wg_raw[1], wg_rounded[:, PACK * N : 2 * PACK * N])
+        wg_codes, wg_scales = quantize(wg_rounded, "wg")
         z1 = {0: held([P, PACK, HALF], F32, "z1_0", "slot_z1_0")}
-        sum_children([(tile, 0) for tile in range(4, 8)], z1)
+        sum_children([(tile, 0) for tile in range(4, 8)], lambda s, half: z1[half][:, s, :])
 
-        w2_mx = [
-            quantize(round_weight(nc.scalar.copy, w2_raw[0], "w2_bf0", "w2_bf0"), "w2_0"),
-            quantize(round_weight(nc.scalar.copy, w2_raw[1], "w2_bf1", "slot_z1_1"), "w2_1"),
-        ]
+        w2_rounded = held([P, 2 * PACK * N], BF16, "w2_rounded", "slot_z1_1")
+        for b in range(2):
+            round_weight(nc.scalar.copy, w2_raw[b][:], w2_rounded[:, b * PACK * N : (b + 1) * PACK * N])
+        w2_codes, w2_scales = quantize(w2_rounded, "w2")
         z1[1] = held([P, PACK, HALF], F32, "z1_1", "slot_z1_1")
-        sum_children([(tile, 1) for tile in range(4, 8)], z1)
+        sum_children([(tile, 1) for tile in range(4, 8)], lambda s, half: z1[half][:, s, :])
 
+        z0_codes, z0_scales = quantize(interleave(nc.scalar.copy, z0, "z0_bf", "z0_bf"), "z0")
         z_mx = {}
         for half in range(2):
-            name = "z0_bf%d" % half
-            z_mx[(0, half)] = quantize(interleave(nc.scalar.copy, z0[half], name, name), name)
+            cols = slice(half * HALF, (half + 1) * HALF)
+            z_mx[(0, half)] = (z0_codes[:, cols], z0_scales[:, cols])
 
         q = [held([P, S], F32, "q%d" % t) for t in range(PACK)]
         for t in range(PACK):
             for j in range(2):
                 acc = psum.tile([P, BANK], F32, name="acc")
                 for a in range(2):
-                    codes, scales = wg_mx[a]
-                    token_pass(acc, codes[:, t * P : (t + 1) * P].bitcast(FP8X4), scales[:, t * P : (t + 1) * P], a, j)
+                    cols = slice(a * N + t * P, a * N + (t + 1) * P)
+                    token_pass(acc, wg_codes[:, cols].bitcast(FP8X4), wg_scales[:, cols], a, j)
                 nc.scalar.copy(q[t][:, j * BANK : (j + 1) * BANK], acc[:])
 
         gate = []
@@ -235,14 +236,14 @@ def tile_list_syntax_pair_compose_kernel(
                 for e in range(2):
                     t = 2 * pair + e
                     for b in range(2):
-                        w_codes, w_scales = w2_mx[b]
+                        cols = slice(b * N + t * P, b * N + (t + 1) * P)
                         z_codes, z_scales = z_mx[(b, half)]
                         nc.tensor.matmul_mx(
                             out=acc[:, e, :],
-                            lhsT=w_codes[:, t * P : (t + 1) * P].bitcast(FP8X4),
-                            lhsT_scale=w_scales[:, t * P : (t + 1) * P],
-                            rhs=z_codes[:].bitcast(FP8X4),
-                            rhs_scale=z_scales[:],
+                            lhsT=w2_codes[:, cols].bitcast(FP8X4),
+                            lhsT_scale=w2_scales[:, cols],
+                            rhs=z_codes.bitcast(FP8X4),
+                            rhs_scale=z_scales,
                             start=(b == 0),
                             stop=(b == 1),
                         )
@@ -256,7 +257,8 @@ def tile_list_syntax_pair_compose_kernel(
         gate_rows(0, "logits0")
         gate_rows(1, "logits1")
         for half in range(2):
-            z_mx[(1, half)] = quantize(z1_rounded[half], "z1_bf%d" % half)
+            z1_codes, z1_scales = quantize(z1_rounded[half], "z1_%d" % half)
+            z_mx[(1, half)] = (z1_codes[:], z1_scales[:])
             gate_rows(2 + half, "slot_logits%d" % (2 + half))
             compose(half)
 

@@ -114,10 +114,10 @@ def tile_list_syntax_pair_compose_kernel(
             for s in range(PACK):
                 nc.sync.dma_start(w2_raw[b][:, s, :], rows[s])
 
-        def round_weight(copy, raw, rounded):
+        def round_weight(copy, raw, rounded, pairs=slice(0, 2)):
             copy(
-                rounded.rearrange("p (u e m j) -> p u m j e", u=2, e=2, j=PACK),
-                raw.rearrange("p j (m u e) -> p u m j e", u=2, e=2),
+                rounded.rearrange("p (u e m j) -> p u m j e", u=2, e=2, j=PACK)[:, pairs],
+                raw.rearrange("p j (m u e) -> p u m j e", u=2, e=2)[:, pairs],
             )
 
         def quantize(rounded, name):
@@ -128,7 +128,7 @@ def tile_list_syntax_pair_compose_kernel(
             return codes, scales
 
         wg_rounded = held([P, 2 * PACK * N], BF16, "wg_rounded", "slot_z1_0")
-        round_weight(nc.vector.tensor_copy, wg_raw[0], wg_rounded[:, 0 : PACK * N])
+        round_weight(nc.vector.tensor_copy, wg_raw[0], wg_rounded[:, 0 : PACK * N], slice(0, 1))
 
         def token_pass(acc, codes, scales, a, j):
             nc.tensor.matmul_mx(
@@ -153,62 +153,62 @@ def tile_list_syntax_pair_compose_kernel(
             for j in range(2):
                 h_acc[(tile, j)] = psum.tile([P, BANK], F32, name="acc")
                 h_pass(h_acc[(tile, j)], tile, 0, j)
-        for tile in range(8):
-            for j in range(2):
-                if tile >= 4:
-                    h_acc[(tile, j)] = psum.tile([P, BANK], F32, name="acc")
-                    h_pass(h_acc[(tile, j)], tile, 0, j)
-                h_pass(h_acc[(tile, j)], tile, 1, j)
-                nc.scalar.copy(h[tile][:, j * BANK : (j + 1) * BANK], h_acc[(tile, j)][:])
-
-        def node_slice(pos, half):
-            return pos[:, half * (HALF // 16) : (half + 1) * (HALF // 16)]
+        order = [(tile, j) for j in range(2) for tile in range(2)] + [(tile, j) for tile in range(2, 8) for j in range(2)]
+        for tile, j in order:
+            if tile >= 4:
+                h_acc[(tile, j)] = psum.tile([P, BANK], F32, name="acc")
+                h_pass(h_acc[(tile, j)], tile, 0, j)
+            h_pass(h_acc[(tile, j)], tile, 1, j)
+            nc.scalar.copy(h[tile][:, j * BANK : (j + 1) * BANK], h_acc[(tile, j)][:])
 
         def sum_children(units, z):
             first = []
             for n in range(len(units) + 1):
                 if n < len(units):
-                    tile, half = units[n]
-                    child = ring.tile([P, HALF], F32, name="child")
-                    nc.vector.tensor_copy(child[:], h[tile][:].indirect(node_slice(pos1_sb, half)))
+                    tile, nodes = units[n]
+                    child = ring.tile([P, nodes.stop - nodes.start], F32, name="child")
+                    entries = slice(nodes.start // 16, nodes.stop // 16)
+                    nc.vector.tensor_copy(child[:], h[tile][:].indirect(pos1_sb[:, entries]))
                     first.append(child)
                 if n > 0:
-                    tile, half = units[n - 1]
+                    tile, nodes = units[n - 1]
+                    entries = slice(nodes.start // 16, nodes.stop // 16)
                     nc.vector.tensor_tensor(
-                        z(tile % PACK, half), h[tile][:].indirect(node_slice(pos2_sb, half)), first[n - 1][:], ADD
+                        z[:, tile % PACK, nodes], h[tile][:].indirect(pos2_sb[:, entries]), first[n - 1][:], ADD
                     )
 
-        def interleave(copy, rows, name, tag):
-            rounded = held([P, PACK * rows.shape[2]], BF16, name, tag)
+        def interleave(copy, rows, rounded):
             copy(
-                rounded[:].rearrange("p (c i s) -> p c s i", i=2, s=PACK),
-                rows[:].rearrange("p s (c i) -> p c s i", i=2),
+                rounded.rearrange("p (c i s) -> p c s i", i=2, s=PACK),
+                rows.rearrange("p s (c i) -> p c s i", i=2),
             )
-            return rounded
 
+        halves = [slice(0, HALF), slice(HALF, NODES)]
         z0 = held([P, PACK, NODES], F32, "z0")
-        sum_children(
-            [(tile, half) for tile in range(4) for half in range(2)],
-            lambda s, half: z0[:, s, half * HALF : (half + 1) * HALF],
-        )
+        sum_children([(tile, nodes) for tile in range(4) for nodes in halves], z0)
 
+        round_weight(nc.scalar.copy, wg_raw[0], wg_rounded[:, 0 : PACK * N], slice(1, 2))
         round_weight(nc.scalar.copy, wg_raw[1], wg_rounded[:, PACK * N : 2 * PACK * N])
         wg_codes, wg_scales = quantize(wg_rounded, "wg")
-        z1 = {0: held([P, PACK, HALF], F32, "z1_0", "slot_z1_0")}
-        sum_children([(tile, 0) for tile in range(4, 8)], lambda s, half: z1[half][:, s, :])
+        first1 = held([P, PACK, NODES], F32, "first1", "slot_z1_0")
+        for s in range(PACK):
+            nc.vector.tensor_copy(first1[:, s, :], h[PACK + s][:].indirect(pos1_sb[:]))
+        z1 = held([P, PACK, NODES], F32, "z1")
+        for nodes in halves:
+            entries = slice(nodes.start // 16, nodes.stop // 16)
+            for s in range(PACK):
+                nc.vector.tensor_tensor(
+                    z1[:, s, nodes], h[PACK + s][:].indirect(pos2_sb[:, entries]), first1[:, s, nodes], ADD
+                )
 
-        w2_rounded = held([P, 2 * PACK * N], BF16, "w2_rounded", "slot_z1_1")
+        w2_rounded = held([P, 2 * PACK * N], BF16, "w2_rounded")
         for b in range(2):
             round_weight(nc.scalar.copy, w2_raw[b][:], w2_rounded[:, b * PACK * N : (b + 1) * PACK * N])
         w2_codes, w2_scales = quantize(w2_rounded, "w2")
-        z1[1] = held([P, PACK, HALF], F32, "z1_1", "slot_z1_1")
-        sum_children([(tile, 1) for tile in range(4, 8)], lambda s, half: z1[half][:, s, :])
-
-        z0_codes, z0_scales = quantize(interleave(nc.scalar.copy, z0, "z0_bf", "z0_bf"), "z0")
-        z_mx = {}
-        for half in range(2):
-            cols = slice(half * HALF, (half + 1) * HALF)
-            z_mx[(0, half)] = (z0_codes[:, cols], z0_scales[:, cols])
+        z0_rounded = held([P, PACK * NODES], BF16, "z0_rounded")
+        interleave(nc.scalar.copy, z0[:], z0_rounded[:])
+        z_mx = [quantize(z0_rounded, "z0")]
+        z1_rounded = held([P, PACK * NODES], BF16, "z1_rounded", "slot_logits")
 
         q = [held([P, S], F32, "q%d" % t) for t in range(PACK)]
         for t in range(PACK):
@@ -219,65 +219,50 @@ def tile_list_syntax_pair_compose_kernel(
                     token_pass(acc, wg_codes[:, cols].bitcast(FP8X4), wg_scales[:, cols], a, j)
                 nc.scalar.copy(q[t][:, j * BANK : (j + 1) * BANK], acc[:])
 
-        gate = []
+        for nodes in halves:
+            interleave(nc.scalar.copy, z1[:, :, nodes], z1_rounded[:, PACK * nodes.start : PACK * nodes.stop])
+        z_mx.append(quantize(z1_rounded, "z1"))
 
-        def gate_rows(t, tag):
-            logits = held([P, NODES], F32, "logits%d" % t, tag)
-            nc.vector.tensor_copy(logits[:], q[t][:].indirect(pos1_sb[:]))
-            gate_t = held([P, NODES], F32, "gate%d" % t)
-            nc.scalar.activation(gate_t[:], logits[:], SIGMOID)
-            gate.append(gate_t)
+        m_acc = [psum.tile([P, NODES], F32, name="acc") for t in range(PACK)]
+        for b in range(2):
+            for t in range(PACK):
+                cols = slice(b * N + t * P, b * N + (t + 1) * P)
+                nc.tensor.matmul_mx(
+                    out=m_acc[t][:],
+                    lhsT=w2_codes[:, cols].bitcast(FP8X4),
+                    lhsT_scale=w2_scales[:, cols],
+                    rhs=z_mx[b][0][:].bitcast(FP8X4),
+                    rhs_scale=z_mx[b][1][:],
+                    start=(b == 0),
+                    stop=(b == 1),
+                )
 
-        tanh_m = {}
+        logits = held([P, PACK, NODES], F32, "logits", "slot_logits")
+        gate = held([P, PACK, NODES], F32, "gate")
+        tanh_m = held([P, PACK, NODES], F32, "tanh_m")
+        for t in range(PACK):
+            nc.vector.tensor_copy(logits[:, t, :], q[t][:].indirect(pos1_sb[:]))
+            nc.scalar.activation(tanh_m[:, t, :], m_acc[t][:], TANH)
+            nc.scalar.activation(gate[:, t, :], logits[:, t, :], SIGMOID)
 
-        def compose(half):
-            for pair in range(2):
-                acc = psum.tile([P, 2, HALF], F32, name="acc")
-                for e in range(2):
-                    t = 2 * pair + e
-                    for b in range(2):
-                        cols = slice(b * N + t * P, b * N + (t + 1) * P)
-                        z_codes, z_scales = z_mx[(b, half)]
-                        nc.tensor.matmul_mx(
-                            out=acc[:, e, :],
-                            lhsT=w2_codes[:, cols].bitcast(FP8X4),
-                            lhsT_scale=w2_scales[:, cols],
-                            rhs=z_codes.bitcast(FP8X4),
-                            rhs_scale=z_scales,
-                            start=(b == 0),
-                            stop=(b == 1),
-                        )
-                squashed = held([P, 2, HALF], F32, "tanh_m%d_%d" % (half, pair))
-                nc.scalar.activation(squashed[:], acc[:], TANH)
-                tanh_m[(half, pair)] = squashed
-
-        z1_rounded = [
-            interleave(nc.scalar.copy, z1[half], "z1_bf%d" % half, "slot_logits%d" % (2 + half)) for half in range(2)
-        ]
-        gate_rows(0, "logits0")
-        gate_rows(1, "logits1")
-        for half in range(2):
-            z1_codes, z1_scales = quantize(z1_rounded[half], "z1_%d" % half)
-            z_mx[(1, half)] = (z1_codes[:], z1_scales[:])
-            gate_rows(2 + half, "slot_logits%d" % (2 + half))
-            compose(half)
+        y = held([P, PACK, NODES], F32, "y")
+        y_rows = out_0.rearrange("(p t) i -> p t i", t=PACK)
+        for t, nodes in [(t, slice(0, NODES)) for t in range(PACK - 1)] + [(PACK - 1, nodes) for nodes in halves]:
+            nc.vector.scalar_tensor_tensor(
+                y[:, t, nodes], tanh_m[:, t, nodes], gain_sb[:, t : t + 1], gate[:, t, nodes], MULT, MULT
+            )
+        for t in range(PACK):
+            nc.sync.dma_start(y_rows[:, t, :], y[:, t, :])
 
         y_scales = held([P, NODES], U8, "y_scales")
-        y_rows = out_0.rearrange("(p t) i -> p t i", t=PACK)
         code_rows = out_1[0].rearrange("p i t -> p (i t)").bitcast(I32)
+        y_rounded = [held([P, PACK * HALF], BF16, "y_rounded%d" % half) for half in range(2)]
+        interleave(nc.scalar.copy, y[:, :, halves[0]], y_rounded[0][:])
+        interleave(nc.vector.tensor_copy, y[:, :, halves[1]], y_rounded[1][:])
         for half in range(2):
-            cols = slice(half * HALF, (half + 1) * HALF)
-            y = held([P, PACK, HALF], F32, "y%d" % half)
-            for t in range(PACK):
-                nc.vector.scalar_tensor_tensor(
-                    y[:, t, :], tanh_m[(half, t // 2)][:, t % 2, :], gain_sb[:, t : t + 1], gate[t][:, cols], MULT, MULT
-                )
-            nc.sync.dma_start(y_rows[:, :, cols], y[:])
-            name = "y_bf%d" % half
-            rounded = interleave(nc.vector.tensor_copy if half else nc.scalar.copy, y, name, name)
             y_codes = held([P, HALF], I32, "y_codes%d" % half)
-            nc.vector.quantize_mx(out=y_codes[:].bitcast(FP8X4), scales=y_scales[:, cols], in_=rounded[:])
-            nc.sync.dma_start(code_rows[:, cols], y_codes[:])
+            nc.vector.quantize_mx(out=y_codes[:].bitcast(FP8X4), scales=y_scales[:, halves[half]], in_=y_rounded[half][:])
+            nc.sync.dma_start(code_rows[:, halves[half]], y_codes[:])
         for quad in range(4):
             queue = nc.scalar if quad % 2 else nc.sync
             queue.dma_start(

@@ -33,7 +33,7 @@ def tile_list_syntax_pair_compose_kernel(
     with ExitStack() as ctx:
         lists = ctx.enter_context(tc.tile_pool(name="lists", bufs=1))
         keep = ctx.enter_context(tc.tile_pool(name="keep", bufs=1))
-        ring = ctx.enter_context(tc.tile_pool(name="ring", bufs=4))
+        ring = ctx.enter_context(tc.tile_pool(name="ring", bufs=2))
         psum = ctx.enter_context(tc.psum_pool(name="psum", bufs=8))
 
         def held(shape, dtype, name, tag=None):
@@ -42,43 +42,35 @@ def tile_list_syntax_pair_compose_kernel(
         offs_sb = lists.tile([P, S // 16], U16, name="offs_sb")
         pos1_sb = lists.tile([P, NODES // 16], U16, name="pos1_sb")
         pos2_sb = lists.tile([P, NODES // 16], U16, name="pos2_sb")
-        nc.sync.dma_start(offs_sb[:], offs)
-        nc.sync.dma_start(pos1_sb[:], pos1)
-        nc.sync.dma_start(pos2_sb[:], pos2)
-
-        w1s_raw = held([P, 2 * H], U8, "w1s_raw")
-        w1s_rows = w1_scales.bitcast(I32).rearrange("a (q r) c -> r q a c", r=4)
-        for r in range(4):
-            nc.sync.dma_start(w1s_raw[r:P:32, :].bitcast(I32).rearrange("q (a c) -> q a c", a=2), w1s_rows[r])
-        word_window = [held([P, T], I32, "word_window0", "slot_w2_0"), held([P, T], I32, "word_window1")]
-        word_rows = [tab_words[a].rearrange("p t i -> p (t i)").bitcast(I32) for a in range(2)]
-        nc.sync.dma_start(word_window[0][:, 0 : T // 2], word_rows[0][:, 0 : T // 2])
-        gain_sb = held([P, PACK], F32, "gain_sb")
-        nc.sync.dma_start(gain_sb[:], gain.rearrange("(p t) -> p t", t=PACK))
 
         scale_window = held([P, T], U8, "scale_window", "slot_wg")
         nc.vector.memset(scale_window[:].bitcast(I32), 0)
+        w1s_raw = held([P, 2 * H], U8, "w1s_raw")
+        nc.gpsimd.memset(w1s_raw[:].bitcast(I32), 0)
+
+        word_window = [held([P, T], I32, "word_window%d" % a, "slot_w2_%d" % a) for a in range(2)]
+        word_rows = [tab_words[a].rearrange("p t i -> p (t i)").bitcast(I32) for a in range(2)]
+        nc.sync.dma_start(word_window[0][:, 0 : T // 2], word_rows[0][:, 0 : T // 2])
+        nc.sync.dma_start(offs_sb[:], offs)
         scale_rows = tab_scales.bitcast(I32).rearrange("a (q r) c -> r q a c", r=4)
         for r in range(4):
             nc.sync.dma_start(scale_window[r:P:16, :].bitcast(I32), scale_rows[r])
         nc.sync.dma_start(word_window[0][:, T // 2 : T], word_rows[0][:, T // 2 : T])
-        w1w_raw = held([P, H], I32, "w1w_raw", "slot_w2_1")
-        nc.sync.dma_start(
-            w1w_raw[:].rearrange("p (a c) -> p a c", a=2), w1_words.bitcast(I32).rearrange("a p c -> p a c")
-        )
+        w1w_rows = w1_words.bitcast(I32).rearrange("a p (b c) -> b p a c", b=2)
+        w1w_raw = [held([P, 2, H // 4], I32, "w1w_raw%d" % b) for b in range(2)]
+        nc.sync.dma_start(w1w_raw[0][:], w1w_rows[0])
+        gain_sb = held([P, PACK], F32, "gain_sb")
+        nc.sync.dma_start(gain_sb[:], gain.rearrange("(p t) -> p t", t=PACK))
+        w1s_rows = w1_scales.bitcast(I32).rearrange("a (q r) c -> r q a c", r=4)
+        for r in range(4):
+            nc.sync.dma_start(w1s_raw[r:P:32, :].bitcast(I32).rearrange("q (a c) -> q a c", a=2), w1s_rows[r])
         nc.sync.dma_start(word_window[1][:], word_rows[1])
+        nc.sync.dma_start(w1w_raw[1][:], w1w_rows[1])
+        nc.sync.dma_start(pos1_sb[:], pos1)
+        nc.sync.dma_start(pos2_sb[:], pos2)
 
         warm = held([P, PACK], F32, "warm")
         nc.scalar.activation(warm[:], gain_sb[:], SIGMOID)
-
-        w1_scale = held([P, 2 * H], U8, "w1_scale")
-        nc.gpsimd.memset(w1_scale[:].bitcast(I32), 0)
-        for quad in range(4):
-            live = slice(32 * quad, 32 * quad + 4)
-            nc.vector.tensor_copy(
-                w1_scale[live, :].bitcast(I32).rearrange("p (ab s g w) -> p ab s g w", ab=4, s=PACK, w=2),
-                w1s_raw[live, :].bitcast(I32).rearrange("p (ab g s w) -> p ab s g w", ab=4, s=PACK, w=2),
-            )
 
         v_scales0 = held([P, S], U8, "v_scales0")
         nc.vector.tensor_copy(v_scales0[:], scale_window[:].indirect(offs_sb[:]))
@@ -90,10 +82,19 @@ def tile_list_syntax_pair_compose_kernel(
         v_words0 = held([P, S], I32, "v_words0")
         nc.vector.tensor_copy(v_words0[:].bitcast(U32), word_window[0][:].bitcast(U32).indirect(offs_sb[:]))
         v_words = {(0, 0): v_words0[:, 0:BANK], (0, 1): v_words0[:, BANK:S]}
-        w1_codes = held([P, 2 * 2 * H], U8, "w1_codes")
+        w1_codes = [held([P, 2 * H], U8, "w1_codes%d" % b) for b in range(2)]
+
+        def deal_w1(b):
+            nc.vector.tensor_copy(
+                w1_codes[b][:].bitcast(I32).rearrange("p (a s g w) -> p a s g w", a=2, s=PACK, w=4),
+                w1w_raw[b][:].rearrange("p a (g s w) -> p a s g w", s=PACK, w=4),
+            )
+
+        deal_w1(0)
+        w1_scale = held([P, 2 * H], U8, "w1_scale")
         nc.vector.tensor_copy(
-            w1_codes[:].bitcast(I32).rearrange("p (ab s g w) -> p ab s g w", ab=4, s=PACK, w=4),
-            w1w_raw[:].rearrange("p (ab g s w) -> p ab s g w", ab=4, s=PACK, w=4),
+            w1_scale[:].bitcast(I32).rearrange("p (ab s g w) -> p ab s g w", ab=4, s=PACK, w=2),
+            w1s_raw[:].bitcast(I32).rearrange("p (ab g s w) -> p ab s g w", ab=4, s=PACK, w=2),
         )
         for j in range(2):
             part = held([P, BANK], I32, "v_words1_%d" % j)
@@ -101,23 +102,29 @@ def tile_list_syntax_pair_compose_kernel(
                 part[:].bitcast(U32), word_window[1][:].bitcast(U32).indirect(offs_sb[:, 32 * j : 32 * (j + 1)])
             )
             v_words[(1, j)] = part[:]
+        deal_w1(1)
 
         wg_both = held([P, 2 * PACK * N], F32, "wg_raw", "slot_wg")
-        wg_raw = [wg_both[:, a * PACK * N : (a + 1) * PACK * N].rearrange("p (j n) -> p j n", j=PACK) for a in range(2)]
+        wg_rows = [wg[a * PASS_K : (a + 1) * PASS_K, :].rearrange("(p j) n -> p j n", j=PACK) for a in range(2)]
+        wg0_raw = [
+            wg_both[:, c * PACK * N // 2 : (c + 1) * PACK * N // 2].rearrange("p (j n) -> p j n", j=PACK)
+            for c in range(2)
+        ]
+        wg1_raw = wg_both[:, PACK * N : 2 * PACK * N].rearrange("p (j n) -> p j n", j=PACK)
+        for c in range(2):
+            nc.sync.dma_start(wg0_raw[c], wg_rows[0][:, :, c * N // 2 : (c + 1) * N // 2])
+        nc.sync.dma_start(wg1_raw, wg_rows[1])
         w2_raw = [held([P, PACK, N], F32, "w2_raw%d" % b, "slot_w2_%d" % b) for b in range(2)]
-        for a in range(2):
-            nc.sync.dma_start(
-                wg_raw[a], wg[a * PASS_K : (a + 1) * PASS_K, :].rearrange("(p j) n -> p j n", j=PACK)
-            )
         for b in range(2):
             rows = w2[b * PASS_K : (b + 1) * PASS_K, :].rearrange("(g s e) n -> s g e n", s=PACK, e=8)
             for s in range(PACK):
                 nc.sync.dma_start(w2_raw[b][:, s, :], rows[s])
 
-        def round_weight(copy, raw, rounded, pairs=slice(0, 2)):
+        def round_weight(copy, raw, rounded, first_m=0):
+            count = raw.shape[2] // PACK
             copy(
-                rounded.rearrange("p (u e m j) -> p u m j e", u=2, e=2, j=PACK)[:, pairs],
-                raw.rearrange("p j (m u e) -> p u m j e", u=2, e=2)[:, pairs],
+                rounded.rearrange("p (u e m j) -> p u m j e", u=2, e=2, j=PACK)[:, :, first_m : first_m + count],
+                raw.rearrange("p j (m u e) -> p u m j e", u=2, e=2),
             )
 
         def quantize(rounded, name):
@@ -127,8 +134,8 @@ def tile_list_syntax_pair_compose_kernel(
             nc.vector.quantize_mx(out=codes[:].bitcast(FP8X4), scales=scales[:], in_=rounded[:])
             return codes, scales
 
-        wg_rounded = held([P, 2 * PACK * N], BF16, "wg_rounded", "slot_z1_0")
-        round_weight(nc.vector.tensor_copy, wg_raw[0], wg_rounded[:, 0 : PACK * N], slice(0, 1))
+        wg_rounded = held([P, 2 * PACK * N], BF16, "wg_rounded")
+        round_weight(nc.vector.tensor_copy, wg0_raw[0], wg_rounded[:, 0 : PACK * N])
 
         def token_pass(acc, codes, scales, a, j):
             nc.tensor.matmul_mx(
@@ -143,9 +150,9 @@ def tile_list_syntax_pair_compose_kernel(
 
         def h_pass(acc, tile, a, j):
             col = a * H + tile * P
-            token_pass(
-                acc, w1_codes[:, 2 * col : 2 * (col + P)].bitcast(FP4X4), w1_scale[:, col : col + P], a, j
-            )
+            word = a * PASS_K + (tile % PACK) * P
+            codes = w1_codes[tile // PACK][:, 2 * word : 2 * (word + P)]
+            token_pass(acc, codes.bitcast(FP4X4), w1_scale[:, col : col + P], a, j)
 
         h = [held([P, S], F32, "h%d" % tile) for tile in range(8)]
         h_acc = {}
@@ -153,53 +160,53 @@ def tile_list_syntax_pair_compose_kernel(
             for j in range(2):
                 h_acc[(tile, j)] = psum.tile([P, BANK], F32, name="acc")
                 h_pass(h_acc[(tile, j)], tile, 0, j)
-        order = [(tile, j) for j in range(2) for tile in range(2)] + [(tile, j) for tile in range(2, 8) for j in range(2)]
-        for tile, j in order:
+
+        def project(tile, j):
             if tile >= 4:
                 h_acc[(tile, j)] = psum.tile([P, BANK], F32, name="acc")
                 h_pass(h_acc[(tile, j)], tile, 0, j)
             h_pass(h_acc[(tile, j)], tile, 1, j)
             nc.scalar.copy(h[tile][:, j * BANK : (j + 1) * BANK], h_acc[(tile, j)][:])
 
-        def sum_children(units, z):
+        for tile, j in [(tile, j) for j in range(2) for tile in range(2)] + [(tile, j) for tile in (2, 3) for j in range(2)]:
+            project(tile, j)
+        round_weight(nc.scalar.copy, wg0_raw[1], wg_rounded[:, 0 : PACK * N], P // 2)
+        round_weight(nc.scalar.copy, wg1_raw, wg_rounded[:, PACK * N : 2 * PACK * N])
+        for tile in range(4, 8):
+            for j in range(2):
+                project(tile, j)
+
+        halves = [slice(0, HALF), slice(HALF, NODES)]
+
+        def entries(nodes):
+            return slice(nodes.start // 16, nodes.stop // 16)
+
+        def sum_children(tiles, z):
+            units = [(tile, nodes) for tile in tiles for nodes in halves]
             first = []
             for n in range(len(units) + 1):
                 if n < len(units):
                     tile, nodes = units[n]
-                    child = ring.tile([P, nodes.stop - nodes.start], F32, name="child")
-                    entries = slice(nodes.start // 16, nodes.stop // 16)
-                    nc.vector.tensor_copy(child[:], h[tile][:].indirect(pos1_sb[:, entries]))
+                    child = ring.tile([P, HALF], F32, name="child")
+                    nc.vector.tensor_copy(child[:], h[tile][:].indirect(pos1_sb[:, entries(nodes)]))
                     first.append(child)
                 if n > 0:
                     tile, nodes = units[n - 1]
-                    entries = slice(nodes.start // 16, nodes.stop // 16)
                     nc.vector.tensor_tensor(
-                        z[:, tile % PACK, nodes], h[tile][:].indirect(pos2_sb[:, entries]), first[n - 1][:], ADD
+                        z[:, tile % PACK, nodes], h[tile][:].indirect(pos2_sb[:, entries(nodes)]), first[n - 1][:], ADD
                     )
 
         def interleave(copy, rows, rounded):
             copy(
-                rounded.rearrange("p (c i s) -> p c s i", i=2, s=PACK),
-                rows.rearrange("p s (c i) -> p c s i", i=2),
+                rounded.rearrange("p (c i s) -> p c s i", i=4, s=PACK),
+                rows.rearrange("p s (c i) -> p c s i", i=4),
             )
 
-        halves = [slice(0, HALF), slice(HALF, NODES)]
         z0 = held([P, PACK, NODES], F32, "z0")
-        sum_children([(tile, nodes) for tile in range(4) for nodes in halves], z0)
-
-        round_weight(nc.scalar.copy, wg_raw[0], wg_rounded[:, 0 : PACK * N], slice(1, 2))
-        round_weight(nc.scalar.copy, wg_raw[1], wg_rounded[:, PACK * N : 2 * PACK * N])
+        sum_children(range(0, 4), z0)
         wg_codes, wg_scales = quantize(wg_rounded, "wg")
-        first1 = held([P, PACK, NODES], F32, "first1", "slot_z1_0")
-        for s in range(PACK):
-            nc.vector.tensor_copy(first1[:, s, :], h[PACK + s][:].indirect(pos1_sb[:]))
         z1 = held([P, PACK, NODES], F32, "z1")
-        for nodes in halves:
-            entries = slice(nodes.start // 16, nodes.stop // 16)
-            for s in range(PACK):
-                nc.vector.tensor_tensor(
-                    z1[:, s, nodes], h[PACK + s][:].indirect(pos2_sb[:, entries]), first1[:, s, nodes], ADD
-                )
+        sum_children(range(4, 8), z1)
 
         w2_rounded = held([P, 2 * PACK * N], BF16, "w2_rounded")
         for b in range(2):
@@ -208,7 +215,7 @@ def tile_list_syntax_pair_compose_kernel(
         z0_rounded = held([P, PACK * NODES], BF16, "z0_rounded")
         interleave(nc.scalar.copy, z0[:], z0_rounded[:])
         z_mx = [quantize(z0_rounded, "z0")]
-        z1_rounded = held([P, PACK * NODES], BF16, "z1_rounded", "slot_logits")
+        z1_rounded = held([P, PACK * NODES], BF16, "z1_rounded", "slot_logits1")
 
         q = [held([P, S], F32, "q%d" % t) for t in range(PACK)]
         for t in range(PACK):
@@ -219,9 +226,14 @@ def tile_list_syntax_pair_compose_kernel(
                     token_pass(acc, wg_codes[:, cols].bitcast(FP8X4), wg_scales[:, cols], a, j)
                 nc.scalar.copy(q[t][:, j * BANK : (j + 1) * BANK], acc[:])
 
-        for nodes in halves:
-            interleave(nc.scalar.copy, z1[:, :, nodes], z1_rounded[:, PACK * nodes.start : PACK * nodes.stop])
+        interleave(nc.scalar.copy, z1[:], z1_rounded[:])
+        logits = [held([P, PACK, HALF], F32, "logits0")]
+        for t in range(PACK):
+            nc.vector.tensor_copy(logits[0][:, t, :], q[t][:].indirect(pos1_sb[:, entries(halves[0])]))
         z_mx.append(quantize(z1_rounded, "z1"))
+        logits.append(held([P, PACK, HALF], F32, "logits1", "slot_logits1"))
+        for t in range(PACK):
+            nc.vector.tensor_copy(logits[1][:, t, :], q[t][:].indirect(pos1_sb[:, entries(halves[1])]))
 
         m_acc = [psum.tile([P, NODES], F32, name="acc") for t in range(PACK)]
         for b in range(2):
@@ -237,28 +249,28 @@ def tile_list_syntax_pair_compose_kernel(
                     stop=(b == 1),
                 )
 
-        logits = held([P, PACK, NODES], F32, "logits", "slot_logits")
-        gate = held([P, PACK, NODES], F32, "gate")
+        gate = [held([P, PACK, HALF], F32, "gate%d" % half) for half in range(2)]
         tanh_m = held([P, PACK, NODES], F32, "tanh_m")
+        nc.scalar.activation(gate[0][:], logits[0][:], SIGMOID)
         for t in range(PACK):
-            nc.vector.tensor_copy(logits[:, t, :], q[t][:].indirect(pos1_sb[:]))
             nc.scalar.activation(tanh_m[:, t, :], m_acc[t][:], TANH)
-            nc.scalar.activation(gate[:, t, :], logits[:, t, :], SIGMOID)
+        for pair in range(2):
+            nc.scalar.activation(gate[1][:, 2 * pair : 2 * pair + 2, :], logits[1][:, 2 * pair : 2 * pair + 2, :], SIGMOID)
 
-        y = held([P, PACK, NODES], F32, "y")
         y_rows = out_0.rearrange("(p t) i -> p t i", t=PACK)
-        for t, nodes in [(t, slice(0, NODES)) for t in range(PACK - 1)] + [(PACK - 1, nodes) for nodes in halves]:
-            nc.vector.scalar_tensor_tensor(
-                y[:, t, nodes], tanh_m[:, t, nodes], gain_sb[:, t : t + 1], gate[:, t, nodes], MULT, MULT
-            )
-        for t in range(PACK):
-            nc.sync.dma_start(y_rows[:, t, :], y[:, t, :])
+        y = [held([P, PACK, HALF], F32, "y%d" % half) for half in range(2)]
+        for half in range(2):
+            for t in range(PACK):
+                nc.vector.scalar_tensor_tensor(
+                    y[half][:, t, :], tanh_m[:, t, halves[half]], gain_sb[:, t : t + 1], gate[half][:, t, :], MULT, MULT
+                )
+            nc.sync.dma_start(y_rows[:, :, halves[half]], y[half][:])
 
         y_scales = held([P, NODES], U8, "y_scales")
         code_rows = out_1[0].rearrange("p i t -> p (i t)").bitcast(I32)
         y_rounded = [held([P, PACK * HALF], BF16, "y_rounded%d" % half) for half in range(2)]
-        interleave(nc.scalar.copy, y[:, :, halves[0]], y_rounded[0][:])
-        interleave(nc.vector.tensor_copy, y[:, :, halves[1]], y_rounded[1][:])
+        interleave(nc.scalar.copy, y[0][:], y_rounded[0][:])
+        interleave(nc.vector.tensor_copy, y[1][:], y_rounded[1][:])
         for half in range(2):
             y_codes = held([P, HALF], I32, "y_codes%d" % half)
             nc.vector.quantize_mx(out=y_codes[:].bitcast(FP8X4), scales=y_scales[:, halves[half]], in_=y_rounded[half][:])

@@ -205,28 +205,39 @@ def tile_list_syntax_pair_compose_kernel(
         z0 = held([P, PACK, NODES], F32, "z0")
         sum_children(range(0, 4), z0)
         wg_codes, wg_scales = quantize(wg_rounded, "wg")
-        z1 = held([P, PACK, NODES], F32, "z1")
-        sum_children(range(4, 8), z1)
+        q_acc = {}
+        for t in range(PACK):
+            for j in range(2):
+                q_acc[(t, j)] = psum.tile([P, BANK], F32, name="acc")
+                for a in range(2):
+                    cols = slice(a * N + t * P, a * N + (t + 1) * P)
+                    token_pass(q_acc[(t, j)], wg_codes[:, cols].bitcast(FP8X4), wg_scales[:, cols], a, j)
+        first1 = held([P, PACK, NODES], F32, "first1")
+        for s in range(PACK):
+            nc.vector.tensor_copy(first1[:, s, :], h[PACK + s][:].indirect(pos1_sb[:]))
+        w2_rounded = [held([P, PACK * N], BF16, "w2_rounded0", "slot_z1"), held([P, PACK * N], BF16, "w2_rounded1")]
+        round_weight(nc.scalar.copy, w2_raw[0][:], w2_rounded[0][:])
+        w2_mx = [quantize(w2_rounded[0], "w2_0")]
+        z1 = held([P, PACK, NODES], F32, "z1", "slot_z1")
+        for nodes in halves:
+            for s in range(PACK):
+                second = h[PACK + s][:].indirect(pos2_sb[:, entries(nodes)])
+                nc.vector.tensor_tensor(z1[:, s, nodes], second, first1[:, s, nodes], ADD)
 
-        w2_rounded = held([P, 2 * PACK * N], BF16, "w2_rounded")
-        for b in range(2):
-            round_weight(nc.scalar.copy, w2_raw[b][:], w2_rounded[:, b * PACK * N : (b + 1) * PACK * N])
-        w2_codes, w2_scales = quantize(w2_rounded, "w2")
         z0_rounded = held([P, PACK * NODES], BF16, "z0_rounded")
         interleave(nc.scalar.copy, z0[:], z0_rounded[:])
         z_mx = [quantize(z0_rounded, "z0")]
+        round_weight(nc.scalar.copy, w2_raw[1][:], w2_rounded[1][:])
+        w2_mx.append(quantize(w2_rounded[1], "w2_1"))
         z1_rounded = held([P, PACK * NODES], BF16, "z1_rounded", "slot_logits1")
 
         q = [held([P, S], F32, "q%d" % t) for t in range(PACK)]
         for t in range(PACK):
             for j in range(2):
-                acc = psum.tile([P, BANK], F32, name="acc")
-                for a in range(2):
-                    cols = slice(a * N + t * P, a * N + (t + 1) * P)
-                    token_pass(acc, wg_codes[:, cols].bitcast(FP8X4), wg_scales[:, cols], a, j)
-                nc.scalar.copy(q[t][:, j * BANK : (j + 1) * BANK], acc[:])
+                nc.scalar.copy(q[t][:, j * BANK : (j + 1) * BANK], q_acc[(t, j)][:])
 
-        interleave(nc.scalar.copy, z1[:], z1_rounded[:])
+        for nodes in halves:
+            interleave(nc.scalar.copy, z1[:, :, nodes], z1_rounded[:, PACK * nodes.start : PACK * nodes.stop])
         logits = [held([P, PACK, HALF], F32, "logits0")]
         for t in range(PACK):
             nc.vector.tensor_copy(logits[0][:, t, :], q[t][:].indirect(pos1_sb[:, entries(halves[0])]))
@@ -238,11 +249,11 @@ def tile_list_syntax_pair_compose_kernel(
         m_acc = [psum.tile([P, NODES], F32, name="acc") for t in range(PACK)]
         for b in range(2):
             for t in range(PACK):
-                cols = slice(b * N + t * P, b * N + (t + 1) * P)
+                cols = slice(t * P, (t + 1) * P)
                 nc.tensor.matmul_mx(
                     out=m_acc[t][:],
-                    lhsT=w2_codes[:, cols].bitcast(FP8X4),
-                    lhsT_scale=w2_scales[:, cols],
+                    lhsT=w2_mx[b][0][:, cols].bitcast(FP8X4),
+                    lhsT_scale=w2_mx[b][1][:, cols],
                     rhs=z_mx[b][0][:].bitcast(FP8X4),
                     rhs_scale=z_mx[b][1][:],
                     start=(b == 0),
@@ -250,7 +261,7 @@ def tile_list_syntax_pair_compose_kernel(
                 )
 
         gate = [held([P, PACK, HALF], F32, "gate%d" % half) for half in range(2)]
-        tanh_m = held([P, PACK, NODES], F32, "tanh_m")
+        tanh_m = held([P, PACK, NODES], F32, "tanh_m", "first1")
         nc.scalar.activation(gate[0][:], logits[0][:], SIGMOID)
         for t in range(PACK):
             nc.scalar.activation(tanh_m[:, t, :], m_acc[t][:], TANH)
@@ -264,7 +275,8 @@ def tile_list_syntax_pair_compose_kernel(
                 nc.vector.scalar_tensor_tensor(
                     y[half][:, t, :], tanh_m[:, t, halves[half]], gain_sb[:, t : t + 1], gate[half][:, t, :], MULT, MULT
                 )
-            nc.sync.dma_start(y_rows[:, :, halves[half]], y[half][:])
+                if t % 2:
+                    nc.sync.dma_start(y_rows[:, t - 1 : t + 1, halves[half]], y[half][:, t - 1 : t + 1, :])
 
         y_scales = held([P, NODES], U8, "y_scales")
         code_rows = out_1[0].rearrange("p i t -> p (i t)").bitcast(I32)

@@ -43,44 +43,51 @@ def tile_list_syntax_pair_compose_kernel(
         pos1_sb = lists.tile([P, NODES // 16], U16, name="pos1_sb")
         pos2_sb = lists.tile([P, NODES // 16], U16, name="pos2_sb")
 
-        scale_window = held([P, T], U8, "scale_window", "slot_wg")
+        scale_window = held([P, T], U8, "scale_window")
         nc.vector.memset(scale_window[:].bitcast(I32), 0)
         w1s_raw = held([P, 2 * H], U8, "w1s_raw")
         nc.gpsimd.memset(w1s_raw[:].bitcast(I32), 0)
 
-        word_window = [held([P, T], I32, "word_window%d" % a, "slot_w2_%d" % a) for a in range(2)]
+        word_window = [held([P, T], I32, "word_window%d" % a, "slot_table%d" % a) for a in range(2)]
         word_rows = [tab_words[a].rearrange("p t i -> p (t i)").bitcast(I32) for a in range(2)]
         nc.sync.dma_start(word_window[0][:, 0 : T // 2], word_rows[0][:, 0 : T // 2])
         nc.sync.dma_start(offs_sb[:], offs)
-        scale_rows = tab_scales.bitcast(I32).rearrange("a (q r) c -> r q a c", r=4)
+        scale_rows = tab_scales.bitcast(I32).rearrange("a (q r) c -> r (a q) c", r=4)
         for r in range(4):
-            nc.sync.dma_start(scale_window[r:P:16, :].bitcast(I32), scale_rows[r])
+            nc.sync.dma_start(scale_window[8 * (r % 2) + r // 2 : P : 16, :].bitcast(I32), scale_rows[r])
         nc.sync.dma_start(word_window[0][:, T // 2 : T], word_rows[0][:, T // 2 : T])
         w1w_rows = w1_words.bitcast(I32).rearrange("a p (b c) -> b p a c", b=2)
-        w1w_raw = [held([P, 2, H // 4], I32, "w1w_raw%d" % b) for b in range(2)]
+        w1w_raw = [held([P, 2, H // 4], I32, "w1w_raw0", "slot_wg")]
         nc.sync.dma_start(w1w_raw[0][:], w1w_rows[0])
-        gain_sb = held([P, PACK], F32, "gain_sb")
-        nc.sync.dma_start(gain_sb[:], gain.rearrange("(p t) -> p t", t=PACK))
         w1s_rows = w1_scales.bitcast(I32).rearrange("a (q r) c -> r q a c", r=4)
         for r in range(4):
             nc.sync.dma_start(w1s_raw[r:P:32, :].bitcast(I32).rearrange("q (a c) -> q a c", a=2), w1s_rows[r])
-        nc.sync.dma_start(word_window[1][:], word_rows[1])
-        nc.sync.dma_start(w1w_raw[1][:], w1w_rows[1])
         nc.sync.dma_start(pos1_sb[:], pos1)
+        nc.sync.dma_start(word_window[1][:], word_rows[1])
         nc.sync.dma_start(pos2_sb[:], pos2)
 
         warm = held([P, PACK], F32, "warm")
-        nc.scalar.activation(warm[:], gain_sb[:], SIGMOID)
+        warm_in = held([P, PACK], F32, "warm_in")
+        nc.gpsimd.memset(warm_in[:], 0.0)
+        nc.scalar.activation(warm[:], warm_in[:], SIGMOID)
 
-        v_scales0 = held([P, S], U8, "v_scales0")
-        nc.vector.tensor_copy(v_scales0[:], scale_window[:].indirect(offs_sb[:]))
-        v_scales1 = held([P, S], U8, "v_scales1")
-        nc.gpsimd.memset(v_scales1[96:128, :].bitcast(I32), 0)
-        nc.sync.dma_start(v_scales1[0:112, :].bitcast(I32), v_scales0[16:128, :].bitcast(I32))
-        v_scales = [v_scales0, v_scales1]
+        picked_scales = held([P, S], U8, "picked_scales")
+        nc.vector.tensor_copy(picked_scales[:], scale_window[:].indirect(offs_sb[:]))
+        v_scales = [held([P, S], U8, "v_scales%d" % a) for a in range(2)]
+        nc.gpsimd.memset(v_scales[1][96:128, :].bitcast(I32), 0)
+        for a in (1, 0):
+            for odd in (1, 0):
+                first = 64 * a + 8 * odd
+                count = min(64, P - first)
+                nc.sync.dma_start(
+                    v_scales[a][odd : odd + 2 * count - 1 : 2, :].bitcast(I32),
+                    picked_scales[first : first + count, :].bitcast(I32),
+                )
 
         v_words0 = held([P, S], I32, "v_words0")
         nc.vector.tensor_copy(v_words0[:].bitcast(U32), word_window[0][:].bitcast(U32).indirect(offs_sb[:]))
+        w1w_raw.append(held([P, 2, H // 4], I32, "w1w_raw1", "slot_table0"))
+        nc.sync.dma_start(w1w_raw[1][:], w1w_rows[1])
         v_words = {(0, 0): v_words0[:, 0:BANK], (0, 1): v_words0[:, BANK:S]}
         w1_codes = [held([P, 2 * H], U8, "w1_codes%d" % b) for b in range(2)]
 
@@ -114,7 +121,10 @@ def tile_list_syntax_pair_compose_kernel(
         for c in range(2):
             nc.sync.dma_start(wg0_raw[c], wg_rows[0][:, :, c * N // 2 : (c + 1) * N // 2])
         nc.sync.dma_start(wg1_raw, wg_rows[1])
-        w2_raw = [held([P, PACK, N], F32, "w2_raw%d" % b, "slot_w2_%d" % b) for b in range(2)]
+        gain_sb = held([P, PACK], F32, "gain_sb", "w1s_raw")
+        nc.sync.dma_start(gain_sb[:], gain.rearrange("(p t) -> p t", t=PACK))
+        w2_both = held([P, 2, PACK, N], F32, "w2_raw", "slot_table1")
+        w2_raw = [w2_both[:, b] for b in range(2)]
         for b in range(2):
             rows = w2[b * PASS_K : (b + 1) * PASS_K, :].rearrange("(g s e) n -> s g e n", s=PACK, e=8)
             for s in range(PACK):
@@ -156,19 +166,18 @@ def tile_list_syntax_pair_compose_kernel(
 
         h = [held([P, S], F32, "h%d" % tile) for tile in range(8)]
         h_acc = {}
-        for tile in range(4):
-            for j in range(2):
-                h_acc[(tile, j)] = psum.tile([P, BANK], F32, name="acc")
-                h_pass(h_acc[(tile, j)], tile, 0, j)
+        for j in range(2):
+            h_acc[(0, j)] = psum.tile([P, BANK], F32, name="acc")
+            h_pass(h_acc[(0, j)], 0, 0, j)
 
         def project(tile, j):
-            if tile >= 4:
+            if tile >= 1:
                 h_acc[(tile, j)] = psum.tile([P, BANK], F32, name="acc")
                 h_pass(h_acc[(tile, j)], tile, 0, j)
             h_pass(h_acc[(tile, j)], tile, 1, j)
             nc.scalar.copy(h[tile][:, j * BANK : (j + 1) * BANK], h_acc[(tile, j)][:])
 
-        for tile, j in [(tile, j) for j in range(2) for tile in range(2)] + [(tile, j) for tile in (2, 3) for j in range(2)]:
+        for tile, j in [(tile, j) for tile in range(4) for j in range(2)]:
             project(tile, j)
         round_weight(nc.scalar.copy, wg0_raw[1], wg_rounded[:, 0 : PACK * N], P // 2)
         round_weight(nc.scalar.copy, wg1_raw, wg_rounded[:, PACK * N : 2 * PACK * N])
@@ -216,7 +225,7 @@ def tile_list_syntax_pair_compose_kernel(
         for s in range(PACK):
             nc.vector.tensor_copy(first1[:, s, :], h[PACK + s][:].indirect(pos1_sb[:]))
         w2_rounded = [held([P, PACK * N], BF16, "w2_rounded0", "slot_z1"), held([P, PACK * N], BF16, "w2_rounded1")]
-        round_weight(nc.scalar.copy, w2_raw[0][:], w2_rounded[0][:])
+        round_weight(nc.scalar.copy, w2_raw[0], w2_rounded[0][:])
         w2_mx = [quantize(w2_rounded[0], "w2_0")]
         z1 = held([P, PACK, NODES], F32, "z1", "slot_z1")
         for nodes in halves:
@@ -227,7 +236,7 @@ def tile_list_syntax_pair_compose_kernel(
         z0_rounded = held([P, PACK * NODES], BF16, "z0_rounded")
         interleave(nc.scalar.copy, z0[:], z0_rounded[:])
         z_mx = [quantize(z0_rounded, "z0")]
-        round_weight(nc.scalar.copy, w2_raw[1][:], w2_rounded[1][:])
+        round_weight(nc.scalar.copy, w2_raw[1], w2_rounded[1][:])
         w2_mx.append(quantize(w2_rounded[1], "w2_1"))
         z1_rounded = held([P, PACK * NODES], BF16, "z1_rounded", "slot_logits1")
 

@@ -54,7 +54,7 @@ def tile_list_syntax_pair_compose_kernel(
         nc.sync.dma_start(offs_sb[:], offs)
         scale_rows = tab_scales.bitcast(I32).rearrange("a (q r) c -> r (a q) c", r=4)
         for r in range(4):
-            nc.sync.dma_start(scale_window[8 * (r % 2) + r // 2 : P : 16, :].bitcast(I32), scale_rows[r])
+            nc.sync.dma_start(scale_window[3 + 8 * (r % 2) + r // 2 : P : 16, :].bitcast(I32), scale_rows[r])
         nc.sync.dma_start(word_window[0][:, T // 2 : T], word_rows[0][:, T // 2 : T])
         w1w_rows = w1_words.bitcast(I32).rearrange("a p (b c) -> b p a c", b=2)
         w1w_raw = [held([P, 2, H // 4], I32, "w1w_raw0", "slot_wg")]
@@ -77,8 +77,8 @@ def tile_list_syntax_pair_compose_kernel(
         nc.gpsimd.memset(v_scales[1][96:128, :].bitcast(I32), 0)
         for a in (1, 0):
             for odd in (1, 0):
-                first = 64 * a + 8 * odd
-                count = min(64, P - first)
+                first = 3 + 64 * a + 8 * odd
+                count = min(64, (P - first) // 4 * 4)
                 nc.sync.dma_start(
                     v_scales[a][odd : odd + 2 * count - 1 : 2, :].bitcast(I32),
                     picked_scales[first : first + count, :].bitcast(I32),

@@ -24,6 +24,7 @@ PASS_K = P * PACK
 BANK = 512
 HALF = NODES // 2
 ALIGN = 64
+LEAD = T // 2
 
 
 def tile_list_syntax_pair_compose_kernel(
@@ -45,49 +46,47 @@ def tile_list_syntax_pair_compose_kernel(
 
         scale_window = held([P, T], U8, "scale_window")
         nc.vector.memset(scale_window[:].bitcast(I32), 0)
-        w1s_raw = held([P, 2 * H], U8, "w1s_raw")
-        nc.gpsimd.memset(w1s_raw[:].bitcast(I32), 0)
+        w1s_raw = held([P, H], U8, "w1s_raw")
+        v_scales = [held([P, S], U8, "v_scales%d" % a) for a in range(2)]
+        w1_scale = [held([P, H], U8, "w1_scale%d" % b) for b in range(2)]
+        for plane in [w1s_raw] + v_scales + [w1_scale[1]]:
+            nc.vector.memset(plane[:].bitcast(I32), 0)
 
         word_window = [held([P, T], I32, "word_window%d" % a, "slot_table%d" % a) for a in range(2)]
         word_rows = [tab_words[a].rearrange("p t i -> p (t i)").bitcast(I32) for a in range(2)]
-        nc.sync.dma_start(word_window[0][:, 0 : T // 2], word_rows[0][:, 0 : T // 2])
+        nc.sync.dma_start(word_window[0][:, 0:LEAD], word_rows[0][:, 0:LEAD])
         nc.sync.dma_start(offs_sb[:], offs)
-        scale_rows = tab_scales.bitcast(I32).rearrange("a (q r) c -> r (a q) c", r=4)
+        for a in range(2):
+            nc.sync.dma_start(scale_window[64 * a + 4 : 64 * a + 20, :].bitcast(I32), tab_scales[a].bitcast(I32))
+        w1s_rows = w1_scales.bitcast(I32).rearrange("a q (b c) -> b q a c", b=2)
+        w1s_words = w1s_raw[:].bitcast(I32).rearrange("q (a c) -> q a c", a=2)
+        nc.sync.dma_start(w1s_words[8:24], w1s_rows[1])
+        nc.sync.dma_start(pos1_sb[:], pos1)
+        nc.sync.dma_start(pos2_sb[:], pos2)
+        nc.sync.dma_start(word_window[0][:, LEAD:T], word_rows[0][:, LEAD:T])
         for r in range(4):
-            nc.sync.dma_start(scale_window[3 + 8 * (r % 2) + r // 2 : P : 16, :].bitcast(I32), scale_rows[r])
-        nc.sync.dma_start(word_window[0][:, T // 2 : T], word_rows[0][:, T // 2 : T])
+            nc.sync.dma_start(w1s_words[r:P:32], w1s_rows[0, r:16:4])
         w1w_rows = w1_words.bitcast(I32).rearrange("a p (b c) -> b p a c", b=2)
         w1w_raw = [held([P, 2, H // 4], I32, "w1w_raw0", "slot_wg")]
         nc.sync.dma_start(w1w_raw[0][:], w1w_rows[0])
-        w1s_rows = w1_scales.bitcast(I32).rearrange("a (q r) c -> r q a c", r=4)
-        for r in range(4):
-            nc.sync.dma_start(w1s_raw[r:P:32, :].bitcast(I32).rearrange("q (a c) -> q a c", a=2), w1s_rows[r])
-        nc.sync.dma_start(pos1_sb[:], pos1)
-        nc.sync.dma_start(word_window[1][:], word_rows[1])
-        nc.sync.dma_start(pos2_sb[:], pos2)
-
-        warm = held([P, PACK], F32, "warm")
-        warm_in = held([P, PACK], F32, "warm_in")
-        nc.gpsimd.memset(warm_in[:], 0.0)
-        nc.scalar.activation(warm[:], warm_in[:], SIGMOID)
+        nc.sync.dma_start(word_window[1][:, 0:LEAD], word_rows[1][:, 0:LEAD])
 
         picked_scales = held([P, S], U8, "picked_scales")
         nc.vector.tensor_copy(picked_scales[:], scale_window[:].indirect(offs_sb[:]))
-        v_scales = [held([P, S], U8, "v_scales%d" % a) for a in range(2)]
-        nc.gpsimd.memset(v_scales[1][96:128, :].bitcast(I32), 0)
-        for a in (1, 0):
-            for odd in (1, 0):
-                first = 3 + 64 * a + 8 * odd
-                count = min(64, (P - first) // 4 * 4)
+
+        def move_plane(a):
+            for r in range(4):
                 nc.sync.dma_start(
-                    v_scales[a][odd : odd + 2 * count - 1 : 2, :].bitcast(I32),
-                    picked_scales[first : first + count, :].bitcast(I32),
+                    v_scales[a][r:P:32, :].bitcast(I32),
+                    picked_scales[64 * a + 4 + r : 64 * a + 20 : 4, :].bitcast(I32),
                 )
+
+        move_plane(0)
+        nc.sync.dma_start(word_window[1][:, LEAD:T], word_rows[1][:, LEAD:T])
+        move_plane(1)
 
         v_words0 = held([P, S], I32, "v_words0")
         nc.vector.tensor_copy(v_words0[:].bitcast(U32), word_window[0][:].bitcast(U32).indirect(offs_sb[:]))
-        w1w_raw.append(held([P, 2, H // 4], I32, "w1w_raw1", "slot_table0"))
-        nc.sync.dma_start(w1w_raw[1][:], w1w_rows[1])
         v_words = {(0, 0): v_words0[:, 0:BANK], (0, 1): v_words0[:, BANK:S]}
         w1_codes = [held([P, 2 * H], U8, "w1_codes%d" % b) for b in range(2)]
 
@@ -98,10 +97,9 @@ def tile_list_syntax_pair_compose_kernel(
             )
 
         deal_w1(0)
-        w1_scale = held([P, 2 * H], U8, "w1_scale")
         nc.vector.tensor_copy(
-            w1_scale[:].bitcast(I32).rearrange("p (ab s g w) -> p ab s g w", ab=4, s=PACK, w=2),
-            w1s_raw[:].bitcast(I32).rearrange("p (ab g s w) -> p ab s g w", ab=4, s=PACK, w=2),
+            w1_scale[0][:].bitcast(I32).rearrange("p (a s g w) -> p a s g w", a=2, s=PACK, w=2),
+            w1s_raw[:].bitcast(I32).rearrange("p (a g s w) -> p a s g w", a=2, s=PACK, w=2),
         )
         for j in range(2):
             part = held([P, BANK], I32, "v_words1_%d" % j)
@@ -109,18 +107,21 @@ def tile_list_syntax_pair_compose_kernel(
                 part[:].bitcast(U32), word_window[1][:].bitcast(U32).indirect(offs_sb[:, 32 * j : 32 * (j + 1)])
             )
             v_words[(1, j)] = part[:]
-        deal_w1(1)
 
-        wg_both = held([P, 2 * PACK * N], F32, "wg_raw", "slot_wg")
         wg_rows = [wg[a * PASS_K : (a + 1) * PASS_K, :].rearrange("(p j) n -> p j n", j=PACK) for a in range(2)]
-        wg0_raw = [
-            wg_both[:, c * PACK * N // 2 : (c + 1) * PACK * N // 2].rearrange("p (j n) -> p j n", j=PACK)
-            for c in range(2)
-        ]
-        wg1_raw = wg_both[:, PACK * N : 2 * PACK * N].rearrange("p (j n) -> p j n", j=PACK)
-        for c in range(2):
-            nc.sync.dma_start(wg0_raw[c], wg_rows[0][:, :, c * N // 2 : (c + 1) * N // 2])
-        nc.sync.dma_start(wg1_raw, wg_rows[1])
+        wg_raw = []
+        for a, first, count, tag in ((0, 0, 256, "slot_wg"), (0, 256, 128, "slot_z0"), (0, 384, 128, None), (1, 0, 512, None)):
+            piece = held([P, PACK, count], F32, "wg_raw%d" % len(wg_raw), tag)
+            nc.sync.dma_start(piece[:], wg_rows[a][:, :, first : first + count])
+            wg_raw.append((piece[:], a, first))
+            if len(wg_raw) == 1:
+                w1w_raw.append(held([P, 2, H // 4], I32, "w1w_raw1", "slot_table0"))
+                nc.sync.dma_start(w1w_raw[1][:], w1w_rows[1])
+            if len(wg_raw) == 2:
+                for r in range(4):
+                    nc.sync.dma_start(
+                        w1_scale[1][r:P:32, :].bitcast(I32), w1_scale[0][8 + r : 24 : 4, :].bitcast(I32)
+                    )
         gain_sb = held([P, PACK], F32, "gain_sb", "w1s_raw")
         nc.sync.dma_start(gain_sb[:], gain.rearrange("(p t) -> p t", t=PACK))
         w2_both = held([P, 2, PACK, N], F32, "w2_raw", "slot_table1")
@@ -145,7 +146,13 @@ def tile_list_syntax_pair_compose_kernel(
             return codes, scales
 
         wg_rounded = held([P, 2 * PACK * N], BF16, "wg_rounded")
-        round_weight(nc.vector.tensor_copy, wg0_raw[0], wg_rounded[:, 0 : PACK * N])
+
+        def round_wg(copy, index):
+            raw, a, first = wg_raw[index]
+            round_weight(copy, raw, wg_rounded[:, a * PACK * N : (a + 1) * PACK * N], first // PACK)
+
+        round_wg(nc.vector.tensor_copy, 0)
+        deal_w1(1)
 
         def token_pass(acc, codes, scales, a, j):
             nc.tensor.matmul_mx(
@@ -159,28 +166,31 @@ def tile_list_syntax_pair_compose_kernel(
             )
 
         def h_pass(acc, tile, a, j):
-            col = a * H + tile * P
             word = a * PASS_K + (tile % PACK) * P
             codes = w1_codes[tile // PACK][:, 2 * word : 2 * (word + P)]
-            token_pass(acc, codes.bitcast(FP4X4), w1_scale[:, col : col + P], a, j)
+            token_pass(acc, codes.bitcast(FP4X4), w1_scale[tile // PACK][:, word : word + P], a, j)
 
         h = [held([P, S], F32, "h%d" % tile) for tile in range(8)]
         h_acc = {}
-        for j in range(2):
-            h_acc[(0, j)] = psum.tile([P, BANK], F32, name="acc")
-            h_pass(h_acc[(0, j)], 0, 0, j)
+        early = [(0, 0), (1, 0), (0, 1), (1, 1), (2, 0), (2, 1), (3, 0), (3, 1)]
+        for tile, j in early:
+            h_acc[(tile, j)] = psum.tile([P, BANK], F32, name="acc")
+            h_pass(h_acc[(tile, j)], tile, 0, j)
 
         def project(tile, j):
-            if tile >= 1:
+            if tile >= PACK:
                 h_acc[(tile, j)] = psum.tile([P, BANK], F32, name="acc")
                 h_pass(h_acc[(tile, j)], tile, 0, j)
             h_pass(h_acc[(tile, j)], tile, 1, j)
             nc.scalar.copy(h[tile][:, j * BANK : (j + 1) * BANK], h_acc[(tile, j)][:])
 
-        for tile, j in [(tile, j) for tile in range(4) for j in range(2)]:
+        for tile, j in early[:6]:
             project(tile, j)
-        round_weight(nc.scalar.copy, wg0_raw[1], wg_rounded[:, 0 : PACK * N], P // 2)
-        round_weight(nc.scalar.copy, wg1_raw, wg_rounded[:, PACK * N : 2 * PACK * N])
+        round_wg(nc.scalar.copy, 1)
+        for tile, j in early[6:]:
+            project(tile, j)
+        round_wg(nc.scalar.copy, 2)
+        round_wg(nc.scalar.copy, 3)
         for tile in range(4, 8):
             for j in range(2):
                 project(tile, j)
@@ -190,29 +200,20 @@ def tile_list_syntax_pair_compose_kernel(
         def entries(nodes):
             return slice(nodes.start // 16, nodes.stop // 16)
 
-        def sum_children(tiles, z):
-            units = [(tile, nodes) for tile in tiles for nodes in halves]
-            first = []
-            for n in range(len(units) + 1):
-                if n < len(units):
-                    tile, nodes = units[n]
-                    child = ring.tile([P, HALF], F32, name="child")
-                    nc.vector.tensor_copy(child[:], h[tile][:].indirect(pos1_sb[:, entries(nodes)]))
-                    first.append(child)
-                if n > 0:
-                    tile, nodes = units[n - 1]
-                    nc.vector.tensor_tensor(
-                        z[:, tile % PACK, nodes], h[tile][:].indirect(pos2_sb[:, entries(nodes)]), first[n - 1][:], ADD
-                    )
-
         def interleave(copy, rows, rounded):
             copy(
                 rounded.rearrange("p (c i s) -> p c s i", i=4, s=PACK),
                 rows.rearrange("p s (c i) -> p c s i", i=4),
             )
 
-        z0 = held([P, PACK, NODES], F32, "z0")
-        sum_children(range(0, 4), z0)
+        z0 = held([P, PACK, NODES], F32, "z0", "slot_z0")
+        for pair in ((0, 1), (2, 3)):
+            first = {}
+            for s in pair:
+                first[s] = ring.tile([P, NODES], F32, name="child")
+                nc.vector.tensor_copy(first[s][:], h[s][:].indirect(pos1_sb[:]))
+            for s in pair:
+                nc.vector.tensor_tensor(z0[:, s, :], h[s][:].indirect(pos2_sb[:]), first[s][:], ADD)
         wg_codes, wg_scales = quantize(wg_rounded, "wg")
         q_acc = {}
         for t in range(PACK):
@@ -228,10 +229,10 @@ def tile_list_syntax_pair_compose_kernel(
         round_weight(nc.scalar.copy, w2_raw[0], w2_rounded[0][:])
         w2_mx = [quantize(w2_rounded[0], "w2_0")]
         z1 = held([P, PACK, NODES], F32, "z1", "slot_z1")
-        for nodes in halves:
-            for s in range(PACK):
-                second = h[PACK + s][:].indirect(pos2_sb[:, entries(nodes)])
-                nc.vector.tensor_tensor(z1[:, s, nodes], second, first1[:, s, nodes], ADD)
+        last = PACK - 1
+        for s, nodes in [(s, slice(0, NODES)) for s in range(last)] + [(last, nodes) for nodes in halves]:
+            second = h[PACK + s][:].indirect(pos2_sb[:, entries(nodes)])
+            nc.vector.tensor_tensor(z1[:, s, nodes], second, first1[:, s, nodes], ADD)
 
         z0_rounded = held([P, PACK * NODES], BF16, "z0_rounded")
         interleave(nc.scalar.copy, z0[:], z0_rounded[:])

@@ -56,34 +56,42 @@ def tile_list_syntax_pair_compose_kernel(
         word_rows = [tab_words[a].rearrange("p t i -> p (t i)").bitcast(I32) for a in range(2)]
         nc.sync.dma_start(word_window[0][:, 0:LEAD], word_rows[0][:, 0:LEAD])
         nc.sync.dma_start(offs_sb[:], offs)
-        for a in range(2):
-            nc.sync.dma_start(scale_window[64 * a + 4 : 64 * a + 20, :].bitcast(I32), tab_scales[a].bitcast(I32))
+        nc.sync.dma_start(scale_window[0:P:4, :].bitcast(I32), tab_scales.bitcast(I32).rearrange("a q c -> (a q) c"))
         w1s_rows = w1_scales.bitcast(I32).rearrange("a q (b c) -> b q a c", b=2)
         w1s_words = w1s_raw[:].bitcast(I32).rearrange("q (a c) -> q a c", a=2)
-        nc.sync.dma_start(w1s_words[8:24], w1s_rows[1])
-        nc.sync.dma_start(pos1_sb[:], pos1)
-        nc.sync.dma_start(pos2_sb[:], pos2)
-        nc.sync.dma_start(word_window[0][:, LEAD:T], word_rows[0][:, LEAD:T])
+        nc.sync.dma_start(w1s_words[4:P:8], w1s_rows[1])
         for r in range(4):
+            if r == 3:
+                nc.sync.dma_start(word_window[0][:, LEAD:T], word_rows[0][:, LEAD:T])
             nc.sync.dma_start(w1s_words[r:P:32], w1s_rows[0, r:16:4])
         w1w_rows = w1_words.bitcast(I32).rearrange("a p (b c) -> b p a c", b=2)
-        w1w_raw = [held([P, 2, H // 4], I32, "w1w_raw0", "slot_wg")]
+        w1w_raw = [held([P, 2, H // 4], I32, "w1w_raw0")]
         nc.sync.dma_start(w1w_raw[0][:], w1w_rows[0])
         nc.sync.dma_start(word_window[1][:, 0:LEAD], word_rows[1][:, 0:LEAD])
 
         picked_scales = held([P, S], U8, "picked_scales")
         nc.vector.tensor_copy(picked_scales[:], scale_window[:].indirect(offs_sb[:]))
 
-        def move_plane(a):
-            for r in range(4):
+        def move_rows(a, rows):
+            for r in rows:
                 nc.sync.dma_start(
                     v_scales[a][r:P:32, :].bitcast(I32),
-                    picked_scales[64 * a + 4 + r : 64 * a + 20 : 4, :].bitcast(I32),
+                    picked_scales[64 * a + 4 * r : 64 * (a + 1) : 16, :].bitcast(I32),
                 )
 
-        move_plane(0)
+        wg_rows = [wg[a * PASS_K : (a + 1) * PASS_K, :].rearrange("(p j) n -> p j n", j=PACK) for a in range(2)]
+        wg_raw = {}
+
+        def load_wg(name, a, first, count, tag=None):
+            piece = held([P, PACK, count], F32, name, tag)
+            nc.sync.dma_start(piece[:], wg_rows[a][:, :, first : first + count])
+            wg_raw[name] = (piece[:], a, first)
+
+        move_rows(0, range(4))
         nc.sync.dma_start(word_window[1][:, LEAD:T], word_rows[1][:, LEAD:T])
-        move_plane(1)
+        move_rows(1, range(1))
+        load_wg("wg_a", 0, 0, 256)
+        move_rows(1, range(1, 4))
 
         v_words0 = held([P, S], I32, "v_words0")
         nc.vector.tensor_copy(v_words0[:].bitcast(U32), word_window[0][:].bitcast(U32).indirect(offs_sb[:]))
@@ -108,20 +116,15 @@ def tile_list_syntax_pair_compose_kernel(
             )
             v_words[(1, j)] = part[:]
 
-        wg_rows = [wg[a * PASS_K : (a + 1) * PASS_K, :].rearrange("(p j) n -> p j n", j=PACK) for a in range(2)]
-        wg_raw = []
-        for a, first, count, tag in ((0, 0, 256, "slot_wg"), (0, 256, 128, "slot_z0"), (0, 384, 128, None), (1, 0, 512, None)):
-            piece = held([P, PACK, count], F32, "wg_raw%d" % len(wg_raw), tag)
-            nc.sync.dma_start(piece[:], wg_rows[a][:, :, first : first + count])
-            wg_raw.append((piece[:], a, first))
-            if len(wg_raw) == 1:
-                w1w_raw.append(held([P, 2, H // 4], I32, "w1w_raw1", "slot_table0"))
-                nc.sync.dma_start(w1w_raw[1][:], w1w_rows[1])
-            if len(wg_raw) == 2:
-                for r in range(4):
-                    nc.sync.dma_start(
-                        w1_scale[1][r:P:32, :].bitcast(I32), w1_scale[0][8 + r : 24 : 4, :].bitcast(I32)
-                    )
+        w1w_raw.append(held([P, 2, H // 4], I32, "w1w_raw1"))
+        nc.sync.dma_start(w1w_raw[1][:], w1w_rows[1])
+        load_wg("wg_b", 0, 256, 128, "slot_z0")
+        nc.sync.dma_start(pos1_sb[:], pos1)
+        load_wg("wg_d", 1, 0, 512, "slot_table0")
+        nc.sync.dma_start(pos2_sb[:], pos2)
+        for r in range(4):
+            nc.sync.dma_start(w1_scale[1][r:P:32, :].bitcast(I32), w1_scale[0][4 + 8 * r : P : 32, :].bitcast(I32))
+        load_wg("wg_c", 0, 384, 128)
         gain_sb = held([P, PACK], F32, "gain_sb", "w1s_raw")
         nc.sync.dma_start(gain_sb[:], gain.rearrange("(p t) -> p t", t=PACK))
         w2_both = held([P, 2, PACK, N], F32, "w2_raw", "slot_table1")
@@ -147,11 +150,11 @@ def tile_list_syntax_pair_compose_kernel(
 
         wg_rounded = held([P, 2 * PACK * N], BF16, "wg_rounded")
 
-        def round_wg(copy, index):
-            raw, a, first = wg_raw[index]
+        def round_wg(copy, name):
+            raw, a, first = wg_raw[name]
             round_weight(copy, raw, wg_rounded[:, a * PACK * N : (a + 1) * PACK * N], first // PACK)
 
-        round_wg(nc.vector.tensor_copy, 0)
+        round_wg(nc.vector.tensor_copy, "wg_a")
         deal_w1(1)
 
         def token_pass(acc, codes, scales, a, j):
@@ -186,11 +189,11 @@ def tile_list_syntax_pair_compose_kernel(
 
         for tile, j in early[:6]:
             project(tile, j)
-        round_wg(nc.scalar.copy, 1)
+        round_wg(nc.scalar.copy, "wg_b")
         for tile, j in early[6:]:
             project(tile, j)
-        round_wg(nc.scalar.copy, 2)
-        round_wg(nc.scalar.copy, 3)
+        round_wg(nc.scalar.copy, "wg_c")
+        round_wg(nc.scalar.copy, "wg_d")
         for tile in range(4, 8):
             for j in range(2):
                 project(tile, j)
@@ -280,11 +283,18 @@ def tile_list_syntax_pair_compose_kernel(
 
         y_rows = out_0.rearrange("(p t) i -> p t i", t=PACK)
         y = [held([P, PACK, HALF], F32, "y%d" % half) for half in range(2)]
+        quarters = [slice(0, HALF // 2), slice(HALF // 2, HALF)]
         for half in range(2):
             for t in range(PACK):
-                nc.vector.scalar_tensor_tensor(
-                    y[half][:, t, :], tanh_m[:, t, halves[half]], gain_sb[:, t : t + 1], gate[half][:, t, :], MULT, MULT
-                )
+                for cols in quarters if (half, t) == (1, last) else [slice(0, HALF)]:
+                    nc.vector.scalar_tensor_tensor(
+                        y[half][:, t, cols],
+                        tanh_m[:, t, halves[half]][:, cols],
+                        gain_sb[:, t : t + 1],
+                        gate[half][:, t, cols],
+                        MULT,
+                        MULT,
+                    )
                 if t % 2:
                     nc.sync.dma_start(y_rows[:, t - 1 : t + 1, halves[half]], y[half][:, t - 1 : t + 1, :])
 
@@ -292,7 +302,8 @@ def tile_list_syntax_pair_compose_kernel(
         code_rows = out_1[0].rearrange("p i t -> p (i t)").bitcast(I32)
         y_rounded = [held([P, PACK * HALF], BF16, "y_rounded%d" % half) for half in range(2)]
         interleave(nc.scalar.copy, y[0][:], y_rounded[0][:])
-        interleave(nc.vector.tensor_copy, y[1][:], y_rounded[1][:])
+        for cols in quarters:
+            interleave(nc.vector.tensor_copy, y[1][:, :, cols], y_rounded[1][:, PACK * cols.start : PACK * cols.stop])
         for half in range(2):
             y_codes = held([P, HALF], I32, "y_codes%d" % half)
             nc.vector.quantize_mx(out=y_codes[:].bitcast(FP8X4), scales=y_scales[:, halves[half]], in_=y_rounded[half][:])

@@ -34,7 +34,6 @@ def tile_list_syntax_pair_compose_kernel(
     with ExitStack() as ctx:
         lists = ctx.enter_context(tc.tile_pool(name="lists", bufs=1))
         keep = ctx.enter_context(tc.tile_pool(name="keep", bufs=1))
-        ring = ctx.enter_context(tc.tile_pool(name="ring", bufs=2))
         psum = ctx.enter_context(tc.psum_pool(name="psum", bufs=8))
 
         def held(shape, dtype, name, tag=None):
@@ -64,9 +63,14 @@ def tile_list_syntax_pair_compose_kernel(
             if r == 3:
                 nc.sync.dma_start(word_window[0][:, LEAD:T], word_rows[0][:, LEAD:T])
             nc.sync.dma_start(w1s_words[r:P:32], w1s_rows[0, r:16:4])
-        w1w_rows = w1_words.bitcast(I32).rearrange("a p (b c) -> b p a c", b=2)
-        w1w_raw = [held([P, 2, H // 4], I32, "w1w_raw0")]
-        nc.sync.dma_start(w1w_raw[0][:], w1w_rows[0])
+        w1w_rows = w1_words.bitcast(I32)
+        w1w_raw = {}
+
+        def load_w1(a, first, count):
+            w1w_raw[(a, first)] = held([P, count * H // 4], I32, "w1w_raw%d_%d" % (a, first))
+            nc.sync.dma_start(w1w_raw[(a, first)][:], w1w_rows[a][:, first * H // 4 : (first + count) * H // 4])
+
+        load_w1(0, 0, 1)
         nc.sync.dma_start(word_window[1][:, 0:LEAD], word_rows[1][:, 0:LEAD])
 
         picked_scales = held([P, S], U8, "picked_scales")
@@ -89,42 +93,48 @@ def tile_list_syntax_pair_compose_kernel(
 
         move_rows(0, range(4))
         nc.sync.dma_start(word_window[1][:, LEAD:T], word_rows[1][:, LEAD:T])
-        move_rows(1, range(1))
-        load_wg("wg_a", 0, 0, 256)
-        move_rows(1, range(1, 4))
+        load_w1(1, 0, 2)
+        move_rows(1, range(4))
+        load_wg("wg_a", 0, 0, 384, "child0")
+        load_wg("wg_b", 0, 384, 128, "slot_z0")
+        load_w1(0, 1, 1)
 
         v_words0 = held([P, S], I32, "v_words0")
         nc.vector.tensor_copy(v_words0[:].bitcast(U32), word_window[0][:].bitcast(U32).indirect(offs_sb[:]))
         v_words = {(0, 0): v_words0[:, 0:BANK], (0, 1): v_words0[:, BANK:S]}
-        w1_codes = [held([P, 2 * H], U8, "w1_codes%d" % b) for b in range(2)]
+        w1_codes = {}
 
-        def deal_w1(b):
-            nc.vector.tensor_copy(
-                w1_codes[b][:].bitcast(I32).rearrange("p (a s g w) -> p a s g w", a=2, s=PACK, w=4),
-                w1w_raw[b][:].rearrange("p a (g s w) -> p a s g w", s=PACK, w=4),
+        def deal_w1(copy, a, first, count, words):
+            codes = held([P, count * H], U8, "w1_codes%d_%d" % (a, first))
+            copy(
+                codes[:].bitcast(words).rearrange("p (b s g w) -> p b s g w", b=count, s=PACK, w=4),
+                w1w_raw[(a, first)][:].bitcast(words).rearrange("p (b g s w) -> p b s g w", b=count, s=PACK, w=4),
             )
+            for b in range(count):
+                w1_codes[(a, first + b)] = codes[:, b * H : (b + 1) * H]
 
-        deal_w1(0)
+        deal_w1(nc.vector.tensor_copy, 0, 0, 1, I32)
+        deal_w1(nc.scalar.copy, 1, 0, 2, U32)
+        deal_w1(nc.gpsimd.tensor_copy, 0, 1, 1, I32)
         nc.vector.tensor_copy(
             w1_scale[0][:].bitcast(I32).rearrange("p (a s g w) -> p a s g w", a=2, s=PACK, w=2),
             w1s_raw[:].bitcast(I32).rearrange("p (a g s w) -> p a s g w", a=2, s=PACK, w=2),
         )
         for j in range(2):
             part = held([P, BANK], I32, "v_words1_%d" % j)
-            nc.vector.tensor_copy(
-                part[:].bitcast(U32), word_window[1][:].bitcast(U32).indirect(offs_sb[:, 32 * j : 32 * (j + 1)])
-            )
+            for first, count in [(0, BANK)] if j == 0 else [(0, BANK // 2), (BANK // 2, BANK // 2)]:
+                column = (j * BANK + first) // 16
+                nc.vector.tensor_copy(
+                    part[:, first : first + count].bitcast(U32),
+                    word_window[1][:].bitcast(U32).indirect(offs_sb[:, column : column + count // 16]),
+                )
             v_words[(1, j)] = part[:]
 
-        w1w_raw.append(held([P, 2, H // 4], I32, "w1w_raw1"))
-        nc.sync.dma_start(w1w_raw[1][:], w1w_rows[1])
-        load_wg("wg_b", 0, 256, 128, "slot_z0")
         nc.sync.dma_start(pos1_sb[:], pos1)
         load_wg("wg_d", 1, 0, 512, "slot_table0")
         nc.sync.dma_start(pos2_sb[:], pos2)
         for r in range(4):
             nc.sync.dma_start(w1_scale[1][r:P:32, :].bitcast(I32), w1_scale[0][4 + 8 * r : P : 32, :].bitcast(I32))
-        load_wg("wg_c", 0, 384, 128)
         gain_sb = held([P, PACK], F32, "gain_sb", "w1s_raw")
         nc.sync.dma_start(gain_sb[:], gain.rearrange("(p t) -> p t", t=PACK))
         w2_both = held([P, 2, PACK, N], F32, "w2_raw", "slot_table1")
@@ -155,44 +165,45 @@ def tile_list_syntax_pair_compose_kernel(
             round_weight(copy, raw, wg_rounded[:, a * PACK * N : (a + 1) * PACK * N], first // PACK)
 
         round_wg(nc.vector.tensor_copy, "wg_a")
-        deal_w1(1)
 
-        def token_pass(acc, codes, scales, a, j):
+        def token_pass(acc, codes, scales, a, j, first=0, count=BANK):
             nc.tensor.matmul_mx(
                 out=acc[:],
                 lhsT=codes,
                 lhsT_scale=scales,
-                rhs=v_words[(a, j)].bitcast(FP8X4),
-                rhs_scale=v_scales[a][:, j * BANK : (j + 1) * BANK],
+                rhs=v_words[(a, j)][:, first : first + count].bitcast(FP8X4),
+                rhs_scale=v_scales[a][:, j * BANK + first : j * BANK + first + count],
                 start=(a == 0),
                 stop=(a == 1),
             )
 
-        def h_pass(acc, tile, a, j):
+        def h_pass(acc, tile, a, j, first=0, count=BANK):
             word = a * PASS_K + (tile % PACK) * P
-            codes = w1_codes[tile // PACK][:, 2 * word : 2 * (word + P)]
-            token_pass(acc, codes.bitcast(FP4X4), w1_scale[tile // PACK][:, word : word + P], a, j)
+            codes = w1_codes[(a, tile // PACK)][:, 2 * P * (tile % PACK) : 2 * P * (tile % PACK + 1)]
+            token_pass(acc, codes.bitcast(FP4X4), w1_scale[tile // PACK][:, word : word + P], a, j, first, count)
 
         h = [held([P, S], F32, "h%d" % tile) for tile in range(8)]
         h_acc = {}
-        early = [(0, 0), (1, 0), (0, 1), (1, 1), (2, 0), (2, 1), (3, 0), (3, 1)]
-        for tile, j in early:
-            h_acc[(tile, j)] = psum.tile([P, BANK], F32, name="acc")
-            h_pass(h_acc[(tile, j)], tile, 0, j)
+        whole, low, high = (0, BANK), (0, BANK // 2), (BANK // 2, BANK // 2)
+        early = [(0, 0, whole), (0, 1, low), (0, 1, high), (1, 0, whole), (1, 1, whole), (2, 0, whole), (2, 1, whole), (3, 0, whole)]
+        for tile, j, part in early:
+            h_acc[(tile, j, part)] = psum.tile([P, part[1]], F32, name="acc")
+            h_pass(h_acc[(tile, j, part)], tile, 0, j, *part)
 
-        def project(tile, j):
-            if tile >= PACK:
-                h_acc[(tile, j)] = psum.tile([P, BANK], F32, name="acc")
-                h_pass(h_acc[(tile, j)], tile, 0, j)
-            h_pass(h_acc[(tile, j)], tile, 1, j)
-            nc.scalar.copy(h[tile][:, j * BANK : (j + 1) * BANK], h_acc[(tile, j)][:])
+        def project(tile, j, part=whole):
+            if (tile, j, part) not in h_acc:
+                h_acc[(tile, j, part)] = psum.tile([P, BANK], F32, name="acc")
+                h_pass(h_acc[(tile, j, part)], tile, 0, j)
+            h_pass(h_acc[(tile, j, part)], tile, 1, j, *part)
+            first = j * BANK + part[0]
+            nc.scalar.copy(h[tile][:, first : first + part[1]], h_acc[(tile, j, part)][:])
 
-        for tile, j in early[:6]:
-            project(tile, j)
+        for piece in early[:5]:
+            project(*piece)
         round_wg(nc.scalar.copy, "wg_b")
-        for tile, j in early[6:]:
-            project(tile, j)
-        round_wg(nc.scalar.copy, "wg_c")
+        for tile in range(2, 4):
+            for j in range(2):
+                project(tile, j)
         round_wg(nc.scalar.copy, "wg_d")
         for tile in range(4, 8):
             for j in range(2):
@@ -213,7 +224,7 @@ def tile_list_syntax_pair_compose_kernel(
         for pair in ((0, 1), (2, 3)):
             first = {}
             for s in pair:
-                first[s] = ring.tile([P, NODES], F32, name="child")
+                first[s] = held([P, NODES], F32, "child_of%d" % s, "child%d" % (s % 2))
                 nc.vector.tensor_copy(first[s][:], h[s][:].indirect(pos1_sb[:]))
             for s in pair:
                 nc.vector.tensor_tensor(z0[:, s, :], h[s][:].indirect(pos2_sb[:]), first[s][:], ADD)
@@ -237,7 +248,7 @@ def tile_list_syntax_pair_compose_kernel(
             second = h[PACK + s][:].indirect(pos2_sb[:, entries(nodes)])
             nc.vector.tensor_tensor(z1[:, s, nodes], second, first1[:, s, nodes], ADD)
 
-        z0_rounded = held([P, PACK * NODES], BF16, "z0_rounded")
+        z0_rounded = held([P, PACK * NODES], BF16, "z0_rounded", "w1_codes1_0")
         interleave(nc.scalar.copy, z0[:], z0_rounded[:])
         z_mx = [quantize(z0_rounded, "z0")]
         round_weight(nc.scalar.copy, w2_raw[1], w2_rounded[1][:])

@@ -115,14 +115,13 @@ def tile_list_syntax_pair_compose_kernel(
 
         deal_w1(nc.vector.tensor_copy, 0, 0, 1, I32)
         deal_w1(nc.scalar.copy, 1, 0, 2, U32)
-        deal_w1(nc.gpsimd.tensor_copy, 0, 1, 1, I32)
         nc.vector.tensor_copy(
             w1_scale[0][:].bitcast(I32).rearrange("p (a s g w) -> p a s g w", a=2, s=PACK, w=2),
             w1s_raw[:].bitcast(I32).rearrange("p (a g s w) -> p a s g w", a=2, s=PACK, w=2),
         )
         for j in range(2):
             part = held([P, BANK], I32, "v_words1_%d" % j)
-            for first, count in [(0, BANK)] if j == 0 else [(0, BANK // 2), (BANK // 2, BANK // 2)]:
+            for first, count in [(0, BANK // 2), (BANK // 2, BANK // 2)]:
                 column = (j * BANK + first) // 16
                 nc.vector.tensor_copy(
                     part[:, first : first + count].bitcast(U32),
@@ -185,7 +184,7 @@ def tile_list_syntax_pair_compose_kernel(
         h = [held([P, S], F32, "h%d" % tile) for tile in range(8)]
         h_acc = {}
         whole, low, high = (0, BANK), (0, BANK // 2), (BANK // 2, BANK // 2)
-        early = [(0, 0, whole), (0, 1, low), (0, 1, high), (1, 0, whole), (1, 1, whole), (2, 0, whole), (2, 1, whole), (3, 0, whole)]
+        early = [(0, 0, low), (0, 0, high), (1, 0, whole), (0, 1, low), (0, 1, high), (1, 1, whole), (2, 0, whole), (2, 1, whole)]
         for tile, j, part in early:
             h_acc[(tile, j, part)] = psum.tile([P, part[1]], F32, name="acc")
             h_pass(h_acc[(tile, j, part)], tile, 0, j, *part)
@@ -198,9 +197,10 @@ def tile_list_syntax_pair_compose_kernel(
             first = j * BANK + part[0]
             nc.scalar.copy(h[tile][:, first : first + part[1]], h_acc[(tile, j, part)][:])
 
-        for piece in early[:5]:
+        for piece in early[:6]:
             project(*piece)
         round_wg(nc.scalar.copy, "wg_b")
+        deal_w1(nc.scalar.copy, 0, 1, 1, U32)
         for tile in range(2, 4):
             for j in range(2):
                 project(tile, j)

@@ -25,6 +25,7 @@ BANK = 512
 HALF = NODES // 2
 ALIGN = 64
 LEAD = T // 2
+LEAD1 = 5 * T // 8
 
 
 def tile_list_syntax_pair_compose_kernel(
@@ -34,9 +35,12 @@ def tile_list_syntax_pair_compose_kernel(
     with ExitStack() as ctx:
         lists = ctx.enter_context(tc.tile_pool(name="lists", bufs=1))
         keep = ctx.enter_context(tc.tile_pool(name="keep", bufs=1))
+        lap = ctx.enter_context(tc.tile_pool(name="lap", bufs=1))
         psum = ctx.enter_context(tc.psum_pool(name="psum", bufs=8))
 
         def held(shape, dtype, name, tag=None):
+            if isinstance(tag, int):
+                return lap.tile(shape, dtype, name=name, align_bytes=ALIGN, offset=tag)
             return keep.tile(shape, dtype, name=name, tag=tag or name, align_bytes=ALIGN)
 
         offs_sb = lists.tile([P, S // 16], U16, name="offs_sb")
@@ -66,12 +70,13 @@ def tile_list_syntax_pair_compose_kernel(
         w1w_rows = w1_words.bitcast(I32)
         w1w_raw = {}
 
-        def load_w1(a, first, count):
-            w1w_raw[(a, first)] = held([P, count * H // 4], I32, "w1w_raw%d_%d" % (a, first))
+        def load_w1(a, first, count, tag=None):
+            w1w_raw[(a, first)] = held([P, count * H // 4], I32, "w1w_raw%d_%d" % (a, first), tag)
             nc.sync.dma_start(w1w_raw[(a, first)][:], w1w_rows[a][:, first * H // 4 : (first + count) * H // 4])
 
         load_w1(0, 0, 1)
-        nc.sync.dma_start(word_window[1][:, 0:LEAD], word_rows[1][:, 0:LEAD])
+        nc.sync.dma_start(word_window[1][:, 0:LEAD1], word_rows[1][:, 0:LEAD1])
+        nc.sync.dma_start(pos1_sb[:], pos1)
 
         picked_scales = held([P, S], U8, "picked_scales")
         nc.vector.tensor_copy(picked_scales[:], scale_window[:].indirect(offs_sb[:]))
@@ -92,12 +97,12 @@ def tile_list_syntax_pair_compose_kernel(
             wg_raw[name] = (piece[:], a, first)
 
         move_rows(0, range(4))
-        nc.sync.dma_start(word_window[1][:, LEAD:T], word_rows[1][:, LEAD:T])
+        nc.sync.dma_start(word_window[1][:, LEAD1:T], word_rows[1][:, LEAD1:T])
         load_w1(1, 0, 2)
         move_rows(1, range(4))
-        load_wg("wg_a", 0, 0, 384, "child0")
+        load_wg("wg_a", 0, 0, 384, 0)
         load_wg("wg_b", 0, 384, 128, "slot_z0")
-        load_w1(0, 1, 1)
+        load_w1(0, 1, 1, 6144)
 
         v_words0 = held([P, S], I32, "v_words0")
         nc.vector.tensor_copy(v_words0[:].bitcast(U32), word_window[0][:].bitcast(U32).indirect(offs_sb[:]))
@@ -129,9 +134,8 @@ def tile_list_syntax_pair_compose_kernel(
                 )
             v_words[(1, j)] = part[:]
 
-        nc.sync.dma_start(pos1_sb[:], pos1)
-        load_wg("wg_d", 1, 0, 512, "slot_table0")
         nc.sync.dma_start(pos2_sb[:], pos2)
+        load_wg("wg_d", 1, 0, 512, "slot_table0")
         for r in range(4):
             nc.sync.dma_start(w1_scale[1][r:P:32, :].bitcast(I32), w1_scale[0][4 + 8 * r : P : 32, :].bitcast(I32))
         gain_sb = held([P, PACK], F32, "gain_sb", "w1s_raw")
@@ -189,21 +193,29 @@ def tile_list_syntax_pair_compose_kernel(
             h_acc[(tile, j, part)] = psum.tile([P, part[1]], F32, name="acc")
             h_pass(h_acc[(tile, j, part)], tile, 0, j, *part)
 
-        def project(tile, j, part=whole):
+        def empty(tile, j, part, cols):
+            first = j * BANK + part[0] + cols[0]
+            nc.scalar.copy(h[tile][:, first : first + cols[1]], h_acc[(tile, j, part)][:, cols[0] : cols[0] + cols[1]])
+
+        def project(tile, j, part=whole, cols=None):
             if (tile, j, part) not in h_acc:
                 h_acc[(tile, j, part)] = psum.tile([P, BANK], F32, name="acc")
                 h_pass(h_acc[(tile, j, part)], tile, 0, j)
             h_pass(h_acc[(tile, j, part)], tile, 1, j, *part)
-            first = j * BANK + part[0]
-            nc.scalar.copy(h[tile][:, first : first + part[1]], h_acc[(tile, j, part)][:])
+            empty(tile, j, part, cols or (0, part[1]))
 
-        for piece in early[:6]:
-            project(*piece)
+        project(0, 0, low)
+        project(0, 0, high)
+        project(1, 0, whole, low)
+        project(0, 1, low)
+        project(0, 1, high)
+        empty(1, 0, whole, high)
+        project(1, 1)
         round_wg(nc.scalar.copy, "wg_b")
-        deal_w1(nc.scalar.copy, 0, 1, 1, U32)
         for tile in range(2, 4):
             for j in range(2):
                 project(tile, j)
+        deal_w1(nc.scalar.copy, 0, 1, 1, U32)
         round_wg(nc.scalar.copy, "wg_d")
         for tile in range(4, 8):
             for j in range(2):
@@ -224,7 +236,7 @@ def tile_list_syntax_pair_compose_kernel(
         for pair in ((0, 1), (2, 3)):
             first = {}
             for s in pair:
-                first[s] = held([P, NODES], F32, "child_of%d" % s, "child%d" % (s % 2))
+                first[s] = held([P, NODES], F32, "child_of%d" % s, 4 * NODES * s + 512 * (s // 2))
                 nc.vector.tensor_copy(first[s][:], h[s][:].indirect(pos1_sb[:]))
             for s in pair:
                 nc.vector.tensor_tensor(z0[:, s, :], h[s][:].indirect(pos2_sb[:]), first[s][:], ADD)

@@ -55,6 +55,10 @@ def tile_list_syntax_pair_compose_kernel(
         for plane in [w1s_raw] + v_scales + [w1_scale[1]]:
             nc.vector.memset(plane[:].bitcast(I32), 0)
 
+        warm = held([P, 2], F32, "warm")
+        nc.vector.memset(warm[:, 0:1], 0.0)
+        nc.scalar.activation(warm[:, 1:2], warm[:, 0:1], SIGMOID)
+
         word_window = [held([P, T], I32, "word_window%d" % a, "slot_table%d" % a) for a in range(2)]
         word_rows = [tab_words[a].rearrange("p t i -> p (t i)").bitcast(I32) for a in range(2)]
         nc.sync.dma_start(word_window[0][:, 0:LEAD], word_rows[0][:, 0:LEAD])

from contextlib import ExitStack

import concourse.mybir as mybir

K, H, N, T, S, NODES = 1024, 1024, 512, 4096, 1024, 512
FLOPS = 2 * K * H * S + 2 * K * N * S + 2 * H * N * NODES

F32 = mybir.dt.float32
BF16 = mybir.dt.bfloat16
I32 = mybir.dt.int32
U32 = mybir.dt.uint32
U16 = mybir.dt.uint16
U8 = mybir.dt.uint8
FP8X4 = mybir.dt.float8_e4m3fn_x4
FP4X4 = mybir.dt.float4_e2m1fn_x4
MULT = mybir.AluOpType.mult
ADD = mybir.AluOpType.add
SIGMOID = mybir.ActivationFunctionType.Sigmoid
TANH = mybir.ActivationFunctionType.Tanh

P = 128
PACK = 4
PASS_K = P * PACK
BANK = 512
HALF = NODES // 2
ALIGN = 64
LEAD = T // 2
LEAD1 = 5 * T // 8


def tile_list_syntax_pair_compose_kernel(
    tc, tab_words, tab_scales, w1_words, w1_scales, wg, w2, gain, offs, pos1, pos2, out_0, out_1, out_2
):
    nc = tc.nc
    with ExitStack() as ctx:
        lists = ctx.enter_context(tc.tile_pool(name="lists", bufs=1))
        keep = ctx.enter_context(tc.tile_pool(name="keep", bufs=1))
        lap = ctx.enter_context(tc.tile_pool(name="lap", bufs=1))
        psum = ctx.enter_context(tc.psum_pool(name="psum", bufs=8))

        def held(shape, dtype, name, tag=None):
            if isinstance(tag, int):
                return lap.tile(shape, dtype, name=name, align_bytes=ALIGN, offset=tag)
            return keep.tile(shape, dtype, name=name, tag=tag or name, align_bytes=ALIGN)

        offs_sb = lists.tile([P, S // 16], U16, name="offs_sb")
        pos1_sb = lists.tile([P, NODES // 16], U16, name="pos1_sb")
        pos2_sb = lists.tile([P, NODES // 16], U16, name="pos2_sb")

        scale_window = held([P, T], U8, "scale_window")
        nc.vector.memset(scale_window[:].bitcast(I32), 0)
        w1s_raw = held([P, H], U8, "w1s_raw")
        v_scales = [held([P, S], U8, "v_scales%d" % a) for a in range(2)]
        w1_scale = [held([P, H], U8, "w1_scale%d" % b) for b in range(2)]
        for plane in [w1s_raw] + v_scales + [w1_scale[1]]:
            nc.vector.memset(plane[:].bitcast(I32), 0)

        warm = held([P, 2], F32, "warm")
        nc.vector.memset(warm[:, 0:1], 0.0)
        nc.scalar.activation(warm[:, 1:2], warm[:, 0:1], SIGMOID)

        word_window = [held([P, T], I32, "word_window%d" % a, "slot_table%d" % a) for a in range(2)]
        word_rows = [tab_words[a].rearrange("p t i -> p (t i)").bitcast(I32) for a in range(2)]
        nc.sync.dma_start(word_window[0][:, 0:LEAD], word_rows[0][:, 0:LEAD])
        nc.sync.dma_start(offs_sb[:], offs)
        nc.sync.dma_start(scale_window[0:P:4, :].bitcast(I32), tab_scales.bitcast(I32).rearrange("a q c -> (a q) c"))
        w1s_rows = w1_scales.bitcast(I32).rearrange("a q (b c) -> b q a c", b=2)
        w1s_words = w1s_raw[:].bitcast(I32).rearrange("q (a c) -> q a c", a=2)
        nc.sync.dma_start(w1s_words[4:P:8], w1s_rows[1])
        for r in range(4):
            if r == 3:
                nc.sync.dma_start(word_window[0][:, LEAD:T], word_rows[0][:, LEAD:T])
            nc.sync.dma_start(w1s_words[r:P:32], w1s_rows[0, r:16:4])
        w1w_rows = w1_words.bitcast(I32)
        w1w_raw = {}

        def load_w1(a, first, count, tag=None):
            w1w_raw[(a, first)] = held([P, count * H // 4], I32, "w1w_raw%d_%d" % (a, first), tag)
            nc.sync.dma_start(w1w_raw[(a, first)][:], w1w_rows[a][:, first * H // 4 : (first + count) * H // 4])

        load_w1(0, 0, 1)
        nc.sync.dma_start(word_window[1][:, 0:LEAD1], word_rows[1][:, 0:LEAD1])
        nc.sync.dma_start(pos1_sb[:], pos1)

        picked_scales = held([P, S], U8, "picked_scales")
        nc.vector.tensor_copy(picked_scales[:], scale_window[:].indirect(offs_sb[:]))

        def move_rows(a, rows):
            for r in rows:
                nc.sync.dma_start(
                    v_scales[a][r:P:32, :].bitcast(I32),
                    picked_scales[64 * a + 4 * r : 64 * (a + 1) : 16, :].bitcast(I32),
                )

        wg_rows = [wg[a * PASS_K : (a + 1) * PASS_K, :].rearrange("(p j) n -> p j n", j=PACK) for a in range(2)]
        wg_raw = {}

        def load_wg(name, a, first, count, tag=None):
            piece = held([P, PACK, count], F32, name, tag)
            nc.sync.dma_start(piece[:], wg_rows[a][:, :, first : first + count])
            wg_raw[name] = (piece[:], a, first)

        move_rows(0, range(4))
        nc.sync.dma_start(word_window[1][:, LEAD1:T], word_rows[1][:, LEAD1:T])
        load_w1(1, 0, 2)
        move_rows(1, range(4))
        load_wg("wg_a", 0, 0, 384, 0)
        load_wg("wg_b", 0, 384, 128, "slot_z0")
        load_w1(0, 1, 1, 6144)

        v_words0 = held([P, S], I32, "v_words0")
        nc.vector.tensor_copy(v_words0[:].bitcast(U32), word_window[0][:].bitcast(U32).indirect(offs_sb[:]))
        v_words = {(0, 0): v_words0[:, 0:BANK], (0, 1): v_words0[:, BANK:S]}
        w1_codes = {}

        def deal_w1(copy, a, first, count, words):
            codes = held([P, count * H], U8, "w1_codes%d_%d" % (a, first))
            copy(
                codes[:].bitcast(words).rearrange("p (b s g w) -> p b s g w", b=count, s=PACK, w=4),
                w1w_raw[(a, first)][:].bitcast(words).rearrange("p (b g s w) -> p b s g w", b=count, s=PACK, w=4),
            )
            for b in range(count):
                w1_codes[(a, first + b)] = codes[:, b * H : (b + 1) * H]

        deal_w1(nc.vector.tensor_copy, 0, 0, 1, I32)
        deal_w1(nc.scalar.copy, 1, 0, 2, U32)
        nc.vector.tensor_copy(
            w1_scale[0][:].bitcast(I32).rearrange("p (a s g w) -> p a s g w", a=2, s=PACK, w=2),
            w1s_raw[:].bitcast(I32).rearrange("p (a g s w) -> p a s g w", a=2, s=PACK, w=2),
        )
        for j in range(2):
            part = held([P, BANK], I32, "v_words1_%d" % j)
            for first, count in [(0, BANK // 2), (BANK // 2, BANK // 2)]:
                column = (j * BANK + first) // 16
                nc.vector.tensor_copy(
                    part[:, first : first + count].bitcast(U32),
                    word_window[1][:].bitcast(U32).indirect(offs_sb[:, column : column + count // 16]),
                )
            v_words[(1, j)] = part[:]

        nc.sync.dma_start(pos2_sb[:], pos2)
        load_wg("wg_d", 1, 0, 512, "slot_table0")
        for r in range(4):
            nc.sync.dma_start(w1_scale[1][r:P:32, :].bitcast(I32), w1_scale[0][4 + 8 * r : P : 32, :].bitcast(I32))
        gain_sb = held([P, PACK], F32, "gain_sb", "w1s_raw")
        nc.sync.dma_start(gain_sb[:], gain.rearrange("(p t) -> p t", t=PACK))
        w2_both = held([P, 2, PACK, N], F32, "w2_raw", "slot_table1")
        w2_raw = [w2_both[:, b] for b in range(2)]
        for b in range(2):
            rows = w2[b * PASS_K : (b + 1) * PASS_K, :].rearrange("(g s e) n -> s g e n", s=PACK, e=8)
            for s in range(PACK):
                nc.sync.dma_start(w2_raw[b][:, s, :], rows[s])

        def round_weight(copy, raw, rounded, first_m=0):
            count = raw.shape[2] // PACK
            copy(
                rounded.rearrange("p (u e m j) -> p u m j e", u=2, e=2, j=PACK)[:, :, first_m : first_m + count],
                raw.rearrange("p j (m u e) -> p u m j e", u=2, e=2),
            )

        def quantize(rounded, name):
            width = rounded.shape[1] // PACK
            codes = held([P, width], U32, name + "_codes")
            scales = held([P, width], U8, name + "_scales")
            nc.vector.quantize_mx(out=codes[:].bitcast(FP8X4), scales=scales[:], in_=rounded[:])
            return codes, scales

        wg_rounded = held([P, 2 * PACK * N], BF16, "wg_rounded")

        def round_wg(copy, name):
            raw, a, first = wg_raw[name]
            round_weight(copy, raw, wg_rounded[:, a * PACK * N : (a + 1) * PACK * N], first // PACK)

        round_wg(nc.vector.tensor_copy, "wg_a")

        def token_pass(acc, codes, scales, a, j, first=0, count=BANK):
            nc.tensor.matmul_mx(
                out=acc[:],
                lhsT=codes,
                lhsT_scale=scales,
                rhs=v_words[(a, j)][:, first : first + count].bitcast(FP8X4),
                rhs_scale=v_scales[a][:, j * BANK + first : j * BANK + first + count],
                start=(a == 0),
                stop=(a == 1),
            )

        def h_pass(acc, tile, a, j, first=0, count=BANK):
            word = a * PASS_K + (tile % PACK) * P
            codes = w1_codes[(a, tile // PACK)][:, 2 * P * (tile % PACK) : 2 * P * (tile % PACK + 1)]
            token_pass(acc, codes.bitcast(FP4X4), w1_scale[tile // PACK][:, word : word + P], a, j, first, count)

        h = [held([P, S], F32, "h%d" % tile) for tile in range(8)]
        h_acc = {}
        whole, low, high = (0, BANK), (0, BANK // 2), (BANK // 2, BANK // 2)
        early = [(0, 0, low), (0, 0, high), (1, 0, whole), (0, 1, low), (0, 1, high), (1, 1, whole), (2, 0, whole), (2, 1, whole)]
        for tile, j, part in early:
            h_acc[(tile, j, part)] = psum.tile([P, part[1]], F32, name="acc")
            h_pass(h_acc[(tile, j, part)], tile, 0, j, *part)

        def empty(tile, j, part, cols):
            first = j * BANK + part[0] + cols[0]
            nc.scalar.copy(h[tile][:, first : first + cols[1]], h_acc[(tile, j, part)][:, cols[0] : cols[0] + cols[1]])

        def project(tile, j, part=whole, cols=None):
            if (tile, j, part) not in h_acc:
                h_acc[(tile, j, part)] = psum.tile([P, BANK], F32, name="acc")
                h_pass(h_acc[(tile, j, part)], tile, 0, j)
            h_pass(h_acc[(tile, j, part)], tile, 1, j, *part)
            empty(tile, j, part, cols or (0, part[1]))

        project(0, 0, low)
        project(0, 0, high)
        project(1, 0, whole, low)
        project(0, 1, low)
        project(0, 1, high)
        empty(1, 0, whole, high)
        project(1, 1)
        round_wg(nc.scalar.copy, "wg_b")
        for tile in range(2, 4):
            for j in range(2):
                project(tile, j)
        deal_w1(nc.scalar.copy, 0, 1, 1, U32)
        round_wg(nc.scalar.copy, "wg_d")
        for tile in range(4, 8):
            for j in range(2):
                project(tile, j)

        halves = [slice(0, HALF), slice(HALF, NODES)]

        def entries(nodes):
            return slice(nodes.start // 16, nodes.stop // 16)

        def interleave(copy, rows, rounded):
            copy(
                rounded.rearrange("p (c i s) -> p c s i", i=4, s=PACK),
                rows.rearrange("p s (c i) -> p c s i", i=4),
            )

        z0 = held([P, PACK, NODES], F32, "z0", "slot_z0")
        for pair in ((0, 1), (2, 3)):
            first = {}
            for s in pair:
                first[s] = held([P, NODES], F32, "child_of%d" % s, 4 * NODES * s + 512 * (s // 2))
                nc.vector.tensor_copy(first[s][:], h[s][:].indirect(pos1_sb[:]))
            for s in pair:
                nc.vector.tensor_tensor(z0[:, s, :], h[s][:].indirect(pos2_sb[:]), first[s][:], ADD)
        wg_codes, wg_scales = quantize(wg_rounded, "wg")
        q_acc = {}
        for t in range(PACK):
            for j in range(2):
                q_acc[(t, j)] = psum.tile([P, BANK], F32, name="acc")
                for a in range(2):
                    cols = slice(a * N + t * P, a * N + (t + 1) * P)
                    token_pass(q_acc[(t, j)], wg_codes[:, cols].bitcast(FP8X4), wg_scales[:, cols], a, j)
        first1 = held([P, PACK, NODES], F32, "first1")
        for s in range(PACK):
            nc.vector.tensor_copy(first1[:, s, :], h[PACK + s][:].indirect(pos1_sb[:]))
        w2_rounded = [held([P, PACK * N], BF16, "w2_rounded0", "slot_z1"), held([P, PACK * N], BF16, "w2_rounded1")]
        round_weight(nc.scalar.copy, w2_raw[0], w2_rounded[0][:])
        w2_mx = [quantize(w2_rounded[0], "w2_0")]
        z1 = held([P, PACK, NODES], F32, "z1", "slot_z1")
        last = PACK - 1
        for s, nodes in [(s, slice(0, NODES)) for s in range(last)] + [(last, nodes) for nodes in halves]:
            second = h[PACK + s][:].indirect(pos2_sb[:, entries(nodes)])
            nc.vector.tensor_tensor(z1[:, s, nodes], second, first1[:, s, nodes], ADD)

        z0_rounded = held([P, PACK * NODES], BF16, "z0_rounded", "w1_codes1_0")
        interleave(nc.scalar.copy, z0[:], z0_rounded[:])
        z_mx = [quantize(z0_rounded, "z0")]
        round_weight(nc.scalar.copy, w2_raw[1], w2_rounded[1][:])
        w2_mx.append(quantize(w2_rounded[1], "w2_1"))
        z1_rounded = held([P, PACK * NODES], BF16, "z1_rounded", "slot_logits1")

        q = [held([P, S], F32, "q%d" % t) for t in range(PACK)]
        for t in range(PACK):
            for j in range(2):
                nc.scalar.copy(q[t][:, j * BANK : (j + 1) * BANK], q_acc[(t, j)][:])

        for nodes in halves:
            interleave(nc.scalar.copy, z1[:, :, nodes], z1_rounded[:, PACK * nodes.start : PACK * nodes.stop])
        logits = [held([P, PACK, HALF], F32, "logits0")]
        for t in range(PACK):
            nc.vector.tensor_copy(logits[0][:, t, :], q[t][:].indirect(pos1_sb[:, entries(halves[0])]))
        z_mx.append(quantize(z1_rounded, "z1"))
        logits.append(held([P, PACK, HALF], F32, "logits1", "slot_logits1"))
        for t in range(PACK):
            nc.vector.tensor_copy(logits[1][:, t, :], q[t][:].indirect(pos1_sb[:, entries(halves[1])]))

        m_acc = [psum.tile([P, NODES], F32, name="acc") for t in range(PACK)]
        for b in range(2):
            for t in range(PACK):
                cols = slice(t * P, (t + 1) * P)
                nc.tensor.matmul_mx(
                    out=m_acc[t][:],
                    lhsT=w2_mx[b][0][:, cols].bitcast(FP8X4),
                    lhsT_scale=w2_mx[b][1][:, cols],
                    rhs=z_mx[b][0][:].bitcast(FP8X4),
                    rhs_scale=z_mx[b][1][:],
                    start=(b == 0),
                    stop=(b == 1),
                )

        gate = [held([P, PACK, HALF], F32, "gate%d" % half) for half in range(2)]
        tanh_m = held([P, PACK, NODES], F32, "tanh_m", "first1")
        nc.scalar.activation(gate[0][:], logits[0][:], SIGMOID)
        for t in range(PACK):
            nc.scalar.activation(tanh_m[:, t, :], m_acc[t][:], TANH)
        for pair in range(2):
            nc.scalar.activation(gate[1][:, 2 * pair : 2 * pair + 2, :], logits[1][:, 2 * pair : 2 * pair + 2, :], SIGMOID)

        y_rows = out_0.rearrange("(p t) i -> p t i", t=PACK)
        y = [held([P, PACK, HALF], F32, "y%d" % half) for half in range(2)]
        quarters = [slice(0, HALF // 2), slice(HALF // 2, HALF)]
        for half in range(2):
            for t in range(PACK):
                for cols in quarters if (half, t) == (1, last) else [slice(0, HALF)]:
                    nc.vector.scalar_tensor_tensor(
                        y[half][:, t, cols],
                        tanh_m[:, t, halves[half]][:, cols],
                        gain_sb[:, t : t + 1],
                        gate[half][:, t, cols],
                        MULT,
                        MULT,
                    )
                if t % 2:
                    nc.sync.dma_start(y_rows[:, t - 1 : t + 1, halves[half]], y[half][:, t - 1 : t + 1, :])

        y_scales = held([P, NODES], U8, "y_scales")
        code_rows = out_1[0].rearrange("p i t -> p (i t)").bitcast(I32)
        y_rounded = [held([P, PACK * HALF], BF16, "y_rounded%d" % half) for half in range(2)]
        interleave(nc.scalar.copy, y[0][:], y_rounded[0][:])
        for cols in quarters:
            interleave(nc.vector.tensor_copy, y[1][:, :, cols], y_rounded[1][:, PACK * cols.start : PACK * cols.stop])
        for half in range(2):
            y_codes = held([P, HALF], I32, "y_codes%d" % half)
            nc.vector.quantize_mx(out=y_codes[:].bitcast(FP8X4), scales=y_scales[:, halves[half]], in_=y_rounded[half][:])
            nc.sync.dma_start(code_rows[:, halves[half]], y_codes[:])
        for quad in range(4):
            queue = nc.scalar if quad % 2 else nc.sync
            queue.dma_start(
                out_2[0, 4 * quad : 4 * quad + 4, :].bitcast(I32), y_scales[32 * quad : 32 * quad + 4, :].bitcast(I32)
            )
